import numpy as np
import ml_dtypes


def mxq(x, axis, fmt="e4m3"):
    dtype, down = {"e4m3": (ml_dtypes.float8_e4m3fn, 7), "e5m2": (ml_dtypes.float8_e5m2, 14)}[fmt]
    v = np.moveaxis(np.asarray(x, np.float32).astype(ml_dtypes.bfloat16).astype(np.float64), axis, -1)
    blocks = v.reshape(v.shape[:-1] + (-1, 32))
    amax = np.abs(blocks).max(-1, keepdims=True)
    byte = np.maximum(np.where(amax > 0, np.frexp(amax)[1] - 1 + 127, 0) - down, 1)
    scale = np.exp2(byte - 127.0)
    codes = (blocks / scale).astype(np.float32).astype(dtype).astype(np.float64)
    return np.moveaxis((codes * scale).reshape(v.shape), -1, axis)


WIDE = False


def mx_kscale(k):
    if not WIDE:
        return np.ones(k)
    levels = np.array([10, -10, 5, -5, 0])
    if k % 512:
        return np.exp2(np.random.permutation(np.resize(levels, k // 32))).repeat(32)
    a = np.empty((k // 512, 16))
    for p in range(k // 512):
        a[p, :8] = np.random.permutation(np.resize(levels, 8))
        for g in range(8):
            far = levels[np.abs(levels - a[p, g]) >= 10]
            a[p, g + 8] = far[np.random.randint(len(far))]
    return np.exp2(a.ravel()).repeat(32)


def f64(x):
    return np.asarray(x).astype(np.float64)


def striped(idx):
    return np.tile(idx.reshape(-1, 16).T, (8, 1)).astype(np.uint16)


def unstriped(offs):
    return offs[:16].T.reshape(-1).astype(np.int64)


def pack_weight(w):
    k, n = w.shape
    w = f64(np.asarray(w, np.float32).astype(ml_dtypes.bfloat16)).reshape(k // 32, 32, n)
    amax = np.abs(w).max(1)
    byte = np.clip(np.where(amax > 0, np.frexp(amax)[1] - 1 + 127 - 7, 1), 1, 254)
    scaled = (w * np.exp2(127.0 - byte)[:, None, :]).reshape(k, n).astype(np.float32)
    words = np.ascontiguousarray(scaled.reshape(k // 512, 128, 4, n).transpose(0, 1, 3, 2)).astype(ml_dtypes.float8_e4m3fn).view(np.uint8)
    return words, np.ascontiguousarray(byte.astype(np.uint8).reshape(k // 512, 16, n))


def unpack_weight(words, scales):
    g, p, n, _ = words.shape
    vals = np.ascontiguousarray(words).view(ml_dtypes.float8_e4m3fn).astype(np.float64) * np.repeat(np.exp2(scales.astype(np.float64) - 127.0), 8, axis=1)[..., None]
    return vals.transpose(0, 1, 3, 2).reshape(g * 512, n)


def relu(v):
    return np.maximum(v, 0.0)


def sigmoid(v):
    return 1.0 / (1.0 + np.exp(-np.maximum(v, -700.0)))


K, T, S, V, D = 512, 1024, 512, 256, 2


def setup_inputs():
    n = np.random.standard_normal
    s = mx_kscale(K)[:, None]
    packed_xT = pack_weight(n((K, T)) * s)
    packed_eT = pack_weight(n((K, T)) * s)
    return {
        "x_words": packed_xT[0],
        "x_scales": packed_xT[1],
        "e_words": packed_eT[0],
        "e_scales": packed_eT[1],
        "hT": (n((K, V)) / np.sqrt(K) / s).astype(np.float32),
        "tau": (-np.random.uniform(0.5, 1.5, (V, 1))).astype(np.float32),
        "offs": striped(np.random.permutation(T)[:S]),
    }


def reference(x_words, x_scales, e_words, e_scales, hT, tau, offs):
    qp = relu(f64(hT))
    xq = unpack_weight(x_words, x_scales)[:, unstriped(offs)]
    qm = relu(-1.0 * f64(hT))
    e_offs = unpack_weight(e_words, e_scales)[:, unstriped(offs)]
    z = mxq(qm, 0, "e4m3").T @ e_offs
    y = (mxq(qp, 0, "e4m3").T @ xq) - z
    top = y.max(axis=1, keepdims=True)
    mm = y.reshape(len(y), -1, D).max(axis=2)
    return np.exp(y - top) * (sigmoid(2.0 * (np.repeat(mm, D, axis=1) + f64(tau))))

@@ -1,0 +1,163 @@
+from contextlib import ExitStack
+import math
+
+import concourse.mybir as mybir
+
+K, T, S, V = 512, 1024, 512, 256
+FLOPS = 2 * 2 * K * V * S
+
+F32 = mybir.dt.float32
+BF16 = mybir.dt.bfloat16
+I32 = mybir.dt.int32
+U32 = mybir.dt.uint32
+U16 = mybir.dt.uint16
+U8 = mybir.dt.uint8
+FP8X4 = mybir.dt.float8_e4m3fn_x4
+ALU = mybir.AluOpType
+ACT = mybir.ActivationFunctionType
+
+P = 128
+PACK = 4
+HALF = S // 2
+PAIRS = HALF // 2
+LN2 = math.log(2.0)
+
+
+def tile_picked_yquest_gate_p_kernel(tc, x_words, x_scales, e_words, e_scales, hT, tau, offs, out):
+    nc = tc.nc
+    with ExitStack() as ctx:
+        keep = ctx.enter_context(tc.tile_pool(name="keep", bufs=1))
+        psum = ctx.enter_context(tc.psum_pool(name="psum", bufs=1))
+
+        offsets = keep.tile([P, S // 16], U16, name="offsets")
+        nc.sync.dma_start(offsets[:], offs)
+
+        def load_scales(name, src, queue, engine):
+            window = keep.tile([P, T], U8, name=name, tag=name, align_bytes=64)
+            engine.memset(window[:].bitcast(I32), 0)
+            for q in range(4):
+                queue.dma_start(window[32 * q : 32 * q + 4, :].bitcast(I32), src[0, 4 * q : 4 * q + 4, :].bitcast(I32))
+            return window
+
+        def load_words(name, src):
+            window = keep.tile([P, T], I32, name=name, align_bytes=64)
+            nc.sync.dma_start(window[:], src[0].rearrange("p n t -> p (n t)").bitcast(I32))
+            return window
+
+        def gather_words(dst, window, h):
+            nc.vector.tensor_copy(dst[:], window[:].bitcast(U32).indirect(offsets[:, h * HALF // 16 : (h + 1) * HALF // 16]))
+
+        h_raw = keep.tile([P, PACK, V], F32, name="h_raw")
+        nc.sync.dma_start(h_raw[:], hT.rearrange("(p j) t -> p j t", j=PACK))
+        es_win = load_scales("es_win", e_scales, nc.sync, nc.vector)
+        ew_win = load_words("ew_win", e_words)
+        xw_win = load_words("xw_win", x_words)
+        xs_win = load_scales("xs_win", x_scales, nc.sync, nc.gpsimd)
+
+        qm = keep.tile([P, V * PACK], BF16, name="qm", align_bytes=64)
+        qp = keep.tile([P, V * PACK], BF16, name="qp", align_bytes=64)
+        neg_qp = keep.tile([P, V * PACK], BF16, name="neg_qp", align_bytes=64)
+        h_grouped = h_raw[:].rearrange("p j t -> p t j")
+        nc.scalar.activation(qm[:].rearrange("p (t j) -> p t j", j=PACK), h_grouped, ACT.Relu, scale=-1.0)
+        nc.scalar.activation(qp[:].rearrange("p (t j) -> p t j", j=PACK), h_grouped, ACT.Relu)
+        nc.scalar.activation(neg_qp[:], qp[:], ACT.Copy, scale=-1.0)
+        qm_codes = keep.tile([P, V], U32, name="qm_codes", align_bytes=64)
+        qp_codes = keep.tile([P, V], U32, name="qp_codes", align_bytes=64)
+        qm_scales = keep.tile([P, V], U8, name="qm_scales", align_bytes=64)
+        qp_scales = keep.tile([P, V], U8, name="qp_scales", align_bytes=64)
+
+        xs = keep.tile([P, S], U8, name="xs", align_bytes=64)
+        es = keep.tile([P, S], U8, name="es", align_bytes=64)
+        ew = [keep.tile([P, HALF], U32, name=f"ew{h}", align_bytes=64) for h in range(2)]
+        xw = [keep.tile([P, HALF], U32, name="xw0", align_bytes=64)]
+
+        nc.vector.tensor_copy(es[:], es_win[:].indirect(offsets[:]))
+        tau_sb = keep.tile([P, 2, 1], F32, name="tau_sb", tag="es_win", align_bytes=64)
+        with nc.allow_non_contiguous_dma(reason="one threshold a partition"):
+            nc.sync.dma_start(tau_sb[:], tau.rearrange("(r p) o -> p r o", p=P))
+        gate_bias = keep.tile([P, 2, 1], F32, name="gate_bias")
+        nc.scalar.activation(gate_bias[:], tau_sb[:], ACT.Copy, bias=-LN2)
+        gather_words(ew[0], ew_win, 0)
+        nc.vector.quantize_mx(out=qm_codes[:].bitcast(FP8X4), scales=qm_scales[:], in_=qm[:])
+        gather_words(ew[1], ew_win, 1)
+        gather_words(xw[0], xw_win, 0)
+        nc.vector.quantize_mx(out=qp_codes[:].bitcast(FP8X4), scales=qp_scales[:], in_=neg_qp[:])
+        nc.vector.tensor_copy(xs[:], xs_win[:].indirect(offsets[:]))
+        xw.append(keep.tile([P, HALF], U32, name="xw1", tag="xs_win", align_bytes=64))
+        gather_words(xw[1], xw_win, 1)
+
+        banks = {}
+        for h in range(2):
+            cols = slice(h * HALF, (h + 1) * HALF)
+            for r in range(2):
+                rows = slice(r * P, (r + 1) * P)
+                banks[r, h] = psum.tile([P, HALF], F32, name=f"bank{r}{h}")
+                nc.tensor.matmul_mx(out=banks[r, h][:], lhsT=qm_codes[:, rows].bitcast(FP8X4), lhsT_scale=qm_scales[:, rows],
+                                    rhs=ew[h][:].bitcast(FP8X4), rhs_scale=es[:, cols], start=True, stop=False)
+        for h in range(2):
+            cols = slice(h * HALF, (h + 1) * HALF)
+            for r in range(2):
+                rows = slice(r * P, (r + 1) * P)
+                nc.tensor.matmul_mx(out=banks[r, h][:], lhsT=qp_codes[:, rows].bitcast(FP8X4), lhsT_scale=qp_scales[:, rows],
+                                    rhs=xw[h][:].bitcast(FP8X4), rhs_scale=xs[:, cols], start=False, stop=True)
+
+        low = {}
+        gate = {}
+        weight = {}
+        for r in range(2):
+            low[r, 0] = keep.tile([P, PAIRS], F32, name=f"low{r}0")
+            low[r, 1] = keep.tile([P, PAIRS + 1], F32, name=f"low{r}1")
+        lowest = {}
+
+        def pair_min(r, h):
+            bank = banks[r, h]
+            odd = keep.tile([P, PAIRS], F32, name=f"odd{r}{h}")
+            nc.scalar.activation(odd[:], bank[:, 1::2], ACT.Copy, bias=-LN2)
+            nc.vector.scalar_tensor_tensor(low[r, h][:, :PAIRS], bank[:, 0::2], -LN2, odd[:], ALU.add, ALU.min)
+
+        def row_min(r, h):
+            if h == 0:
+                lowest[r, h] = low[r, 1][:, PAIRS:]
+            else:
+                whole = keep.tile([P, 1], F32, name=f"lowest{r}")
+                lowest[r, h] = whole[:]
+            nc.vector.tensor_reduce(lowest[r, h], low[r, h][:], mybir.AxisListType.X, ALU.min)
+
+        def tanh(r, h):
+            gate[r, h] = keep.tile([P, PAIRS], F32, name=f"gate{r}{h}")
+            nc.scalar.activation(gate[r, h][:], low[r, h][:, :PAIRS], ACT.Tanh, bias=gate_bias[:, r, :], scale=-1.0)
+
+        def exp(r, h):
+            weight[r, h] = keep.tile([P, HALF], F32, name=f"weight{r}{h}")
+            nc.scalar.activation(weight[r, h][:], banks[r, h][:], ACT.Exp, bias=lowest[r, h], scale=-1.0)
+
+        for r in range(2):
+            pair_min(r, 0)
+        for r in range(2):
+            row_min(r, 0)
+        for r in range(2):
+            pair_min(r, 1)
+        first_gate = {}
+        for r in range(2):
+            tanh(r, 0)
+            exp(r, 0)
+            first_gate[r] = keep.tile([P, PAIRS], F32, name=f"first_gate{r}")
+            nc.scalar.activation(first_gate[r][:], gate[r, 0][:], ACT.Identity, bias=1.0)
+        for r in range(2):
+            row_min(r, 1)
+        for r in range(2):
+            tanh(r, 1)
+        store_queues = [nc.sync, nc.sync, nc.sync, nc.sync]
+        for r in range(2):
+            shrink = keep.tile([P, 1], F32, name=f"shrink{r}")
+            nc.scalar.activation(shrink[:], lowest[r, 0], ACT.Exp, bias=lowest[r, 1], scale=-1.0)
+            exp(r, 1)
+            for h in range(2):
+                res = keep.tile([P, HALF], F32, name=f"res{r}{h}")
+                res_pairs = res[:].rearrange("p (v d) -> p v d", d=2)
+                weight_pairs = weight[r, h][:].rearrange("p (v d) -> p v d", d=2)
+                if h == 0:
+                    nc.vector.scalar_tensor_tensor(res_pairs, weight_pairs, shrink[:], first_gate[r][:].unsqueeze(2).to_broadcast([P, PAIRS, 2]), ALU.mult, ALU.mult)
+                else:
+                    nc.vector.scalar_tensor_tensor(res_pairs, gate[r, h][:].unsqueeze(2).to_broadcast([P, PAIRS, 2]), 1.0, weight_pairs, ALU.add, ALU.mult)
+                store_queues[2 * r + h].dma_start(out[r * P : (r + 1) * P, h * HALF : (h + 1) * HALF], res[:])

@@ -35,17 +35,14 @@ def tile_picked_yquest_gate_p_kernel(tc, x_words, x_scales, e_words, e_scales, h
         def load_scales(name, src, queue, engine):
             window = keep.tile([P, T], U8, name=name, tag=name, align_bytes=64)
             engine.memset(window[:].bitcast(I32), 0)
-            for q in range(4):
-                queue.dma_start(window[32 * q : 32 * q + 4, :].bitcast(I32), src[0, 4 * q : 4 * q + 4, :].bitcast(I32))
+            for i in range(4):
+                queue.dma_start(window[i:P:32, :].bitcast(I32), src[0, i:16:4, :].bitcast(I32))
             return window
 
         def load_words(name, src):
             window = keep.tile([P, T], I32, name=name, align_bytes=64)
             nc.sync.dma_start(window[:], src[0].rearrange("p n t -> p (n t)").bitcast(I32))
             return window
-
-        def gather_words(dst, window, h):
-            nc.vector.tensor_copy(dst[:], window[:].bitcast(U32).indirect(offsets[:, h * HALF // 16 : (h + 1) * HALF // 16]))
 
         h_raw = keep.tile([P, PACK, V], F32, name="h_raw")
         nc.sync.dma_start(h_raw[:], hT.rearrange("(p j) t -> p j t", j=PACK))
@@ -57,9 +54,9 @@ def tile_picked_yquest_gate_p_kernel(tc, x_words, x_scales, e_words, e_scales, h
         qm = keep.tile([P, V * PACK], BF16, name="qm", align_bytes=64)
         qp = keep.tile([P, V * PACK], BF16, name="qp", align_bytes=64)
         neg_qp = keep.tile([P, V * PACK], BF16, name="neg_qp", align_bytes=64)
-        h_grouped = h_raw[:].rearrange("p j t -> p t j")
-        nc.scalar.activation(qm[:].rearrange("p (t j) -> p t j", j=PACK), h_grouped, ACT.Relu, scale=-1.0)
-        nc.scalar.activation(qp[:].rearrange("p (t j) -> p t j", j=PACK), h_grouped, ACT.Relu)
+        h_walk = h_raw[:].rearrange("p j (c i) -> p c j i", i=4)
+        nc.scalar.activation(qm[:].rearrange("p (c i j) -> p c j i", i=4, j=PACK), h_walk, ACT.Relu, scale=-1.0)
+        nc.scalar.activation(qp[:].rearrange("p (c i j) -> p c j i", i=4, j=PACK), h_walk, ACT.Relu)
         nc.scalar.activation(neg_qp[:], qp[:], ACT.Copy, scale=-1.0)
         qm_codes = keep.tile([P, V], U32, name="qm_codes", align_bytes=64)
         qp_codes = keep.tile([P, V], U32, name="qp_codes", align_bytes=64)
@@ -68,23 +65,19 @@ def tile_picked_yquest_gate_p_kernel(tc, x_words, x_scales, e_words, e_scales, h
 
         xs = keep.tile([P, S], U8, name="xs", align_bytes=64)
         es = keep.tile([P, S], U8, name="es", align_bytes=64)
-        ew = [keep.tile([P, HALF], U32, name=f"ew{h}", align_bytes=64) for h in range(2)]
-        xw = [keep.tile([P, HALF], U32, name="xw0", align_bytes=64)]
+        ew = keep.tile([P, S], U32, name="ew", align_bytes=64)
+        xw = keep.tile([P, S], U32, name="xw", align_bytes=64)
 
         nc.vector.tensor_copy(es[:], es_win[:].indirect(offsets[:]))
         tau_sb = keep.tile([P, 2, 1], F32, name="tau_sb", tag="es_win", align_bytes=64)
         with nc.allow_non_contiguous_dma(reason="one threshold a partition"):
             nc.sync.dma_start(tau_sb[:], tau.rearrange("(r p) o -> p r o", p=P))
-        gate_bias = keep.tile([P, 2, 1], F32, name="gate_bias")
-        nc.scalar.activation(gate_bias[:], tau_sb[:], ACT.Copy, bias=-LN2)
-        gather_words(ew[0], ew_win, 0)
+        nc.vector.tensor_copy(ew[:], ew_win[:].bitcast(U32).indirect(offsets[:]))
         nc.vector.quantize_mx(out=qm_codes[:].bitcast(FP8X4), scales=qm_scales[:], in_=qm[:])
-        gather_words(ew[1], ew_win, 1)
-        gather_words(xw[0], xw_win, 0)
+        nc.vector.tensor_copy(xw[:], xw_win[:].bitcast(U32).indirect(offsets[:]))
         nc.vector.quantize_mx(out=qp_codes[:].bitcast(FP8X4), scales=qp_scales[:], in_=neg_qp[:])
-        nc.vector.tensor_copy(xs[:], xs_win[:].indirect(offsets[:]))
-        xw.append(keep.tile([P, HALF], U32, name="xw1", tag="xs_win", align_bytes=64))
-        gather_words(xw[1], xw_win, 1)
+        for h in range(2):
+            nc.vector.tensor_copy(xs[:, h * HALF : (h + 1) * HALF], xs_win[:].indirect(offsets[:, h * HALF // 16 : (h + 1) * HALF // 16]))
 
         banks = {}
         for h in range(2):
@@ -93,13 +86,13 @@ def tile_picked_yquest_gate_p_kernel(tc, x_words, x_scales, e_words, e_scales, h
                 rows = slice(r * P, (r + 1) * P)
                 banks[r, h] = psum.tile([P, HALF], F32, name=f"bank{r}{h}")
                 nc.tensor.matmul_mx(out=banks[r, h][:], lhsT=qm_codes[:, rows].bitcast(FP8X4), lhsT_scale=qm_scales[:, rows],
-                                    rhs=ew[h][:].bitcast(FP8X4), rhs_scale=es[:, cols], start=True, stop=False)
+                                    rhs=ew[:, cols].bitcast(FP8X4), rhs_scale=es[:, cols], start=True, stop=False)
         for h in range(2):
             cols = slice(h * HALF, (h + 1) * HALF)
             for r in range(2):
                 rows = slice(r * P, (r + 1) * P)
                 nc.tensor.matmul_mx(out=banks[r, h][:], lhsT=qp_codes[:, rows].bitcast(FP8X4), lhsT_scale=qp_scales[:, rows],
-                                    rhs=xw[h][:].bitcast(FP8X4), rhs_scale=xs[:, cols], start=False, stop=True)
+                                    rhs=xw[:, cols].bitcast(FP8X4), rhs_scale=xs[:, cols], start=False, stop=True)
 
         low = {}
         gate = {}
@@ -112,20 +105,22 @@ def tile_picked_yquest_gate_p_kernel(tc, x_words, x_scales, e_words, e_scales, h
         def pair_min(r, h):
             bank = banks[r, h]
             odd = keep.tile([P, PAIRS], F32, name=f"odd{r}{h}")
-            nc.scalar.activation(odd[:], bank[:, 1::2], ACT.Copy, bias=-LN2)
-            nc.vector.scalar_tensor_tensor(low[r, h][:, :PAIRS], bank[:, 0::2], -LN2, odd[:], ALU.add, ALU.min)
+            nc.scalar.copy(odd[:], bank[:, 1::2])
+            nc.vector.tensor_tensor(low[r, h][:, :PAIRS], bank[:, 0::2], odd[:], ALU.min)
 
         def row_min(r, h):
             if h == 0:
                 lowest[r, h] = low[r, 1][:, PAIRS:]
+                nc.vector.tensor_reduce(lowest[r, h], low[r, h][:], mybir.AxisListType.X, ALU.min)
             else:
                 whole = keep.tile([P, 1], F32, name=f"lowest{r}")
+                shifted = keep.tile([P, PAIRS + 1], F32, name=f"shifted{r}")
                 lowest[r, h] = whole[:]
-            nc.vector.tensor_reduce(lowest[r, h], low[r, h][:], mybir.AxisListType.X, ALU.min)
+                nc.vector.tensor_scalar(shifted[:], low[r, h][:], -LN2, None, ALU.add, ALU.min, accum_out=lowest[r, h])
 
         def tanh(r, h):
             gate[r, h] = keep.tile([P, PAIRS], F32, name=f"gate{r}{h}")
-            nc.scalar.activation(gate[r, h][:], low[r, h][:, :PAIRS], ACT.Tanh, bias=gate_bias[:, r, :], scale=-1.0)
+            nc.scalar.activation(gate[r, h][:], low[r, h][:, :PAIRS], ACT.Tanh, bias=tau_sb[:, r, :], scale=-1.0)
 
         def exp(r, h):
             weight[r, h] = keep.tile([P, HALF], F32, name=f"weight{r}{h}")
@@ -142,7 +137,7 @@ def tile_picked_yquest_gate_p_kernel(tc, x_words, x_scales, e_words, e_scales, h
             tanh(r, 0)
             exp(r, 0)
             first_gate[r] = keep.tile([P, PAIRS], F32, name=f"first_gate{r}")
-            nc.scalar.activation(first_gate[r][:], gate[r, 0][:], ACT.Identity, bias=1.0)
+            nc.gpsimd.tensor_scalar(first_gate[r][:], gate[r, 0][:], 1.0, 1.0, ALU.mult, ALU.add)
         for r in range(2):
             row_min(r, 1)
         for r in range(2):

@@ -49,7 +49,7 @@ def tile_picked_yquest_gate_p_kernel(tc, x_words, x_scales, e_words, e_scales, h
         es_win = load_scales("es_win", e_scales, nc.sync, nc.vector)
         ew_win = load_words("ew_win", e_words)
         xw_win = load_words("xw_win", x_words)
-        xs_win = load_scales("xs_win", x_scales, nc.sync, nc.gpsimd)
+        xs_win = load_scales("xs_win", x_scales, nc.sync, nc.vector)
 
         qm = keep.tile([P, V * PACK], BF16, name="qm", align_bytes=64)
         qp = keep.tile([P, V * PACK], BF16, name="qp", align_bytes=64)

@@ -32,11 +32,10 @@ def tile_picked_yquest_gate_p_kernel(tc, x_words, x_scales, e_words, e_scales, h
         offsets = keep.tile([P, S // 16], U16, name="offsets")
         nc.sync.dma_start(offsets[:], offs)
 
-        def load_scales(name, src, queue, engine):
-            window = keep.tile([P, T], U8, name=name, tag=name, align_bytes=64)
-            engine.memset(window[:].bitcast(I32), 0)
-            for i in range(4):
-                queue.dma_start(window[i:P:32, :].bitcast(I32), src[0, i:16:4, :].bitcast(I32))
+        def load_scales(name, src):
+            window = keep.tile([P, T], U8, name=name, align_bytes=64)
+            nc.sync.dma_start(window[P - 16 :, :].bitcast(I32), src[0].bitcast(I32))
+            nc.vector.memset(window[: P - 16, :].bitcast(I32), 0)
             return window
 
         def load_words(name, src):
@@ -44,20 +43,20 @@ def tile_picked_yquest_gate_p_kernel(tc, x_words, x_scales, e_words, e_scales, h
             nc.sync.dma_start(window[:], src[0].rearrange("p n t -> p (n t)").bitcast(I32))
             return window
 
-        h_raw = keep.tile([P, PACK, V], F32, name="h_raw")
+        xs_win = load_scales("xs_win", x_scales)
+        es_win = load_scales("es_win", e_scales)
+        h_raw = keep.tile([P, PACK, V], F32, name="h_raw", tag="h_raw", align_bytes=64)
         nc.sync.dma_start(h_raw[:], hT.rearrange("(p j) t -> p j t", j=PACK))
-        es_win = load_scales("es_win", e_scales, nc.sync, nc.vector)
-        ew_win = load_words("ew_win", e_words)
         xw_win = load_words("xw_win", x_words)
-        xs_win = load_scales("xs_win", x_scales, nc.sync, nc.vector)
+        ew_win = load_words("ew_win", e_words)
 
-        qm = keep.tile([P, V * PACK], BF16, name="qm", align_bytes=64)
-        qp = keep.tile([P, V * PACK], BF16, name="qp", align_bytes=64)
+        qm = keep.tile([P, V * PACK], BF16, name="qm", tag="qm", align_bytes=64)
+        share = ctx.enter_context(tc.tile_pool(name="share", bufs=1))
+        hb = share.tile([P, V * PACK], BF16, name="hb", align_bytes=64, offset=0)
         neg_qp = keep.tile([P, V * PACK], BF16, name="neg_qp", align_bytes=64)
         h_walk = h_raw[:].rearrange("p j (c i) -> p c j i", i=4)
-        nc.scalar.activation(qm[:].rearrange("p (c i j) -> p c j i", i=4, j=PACK), h_walk, ACT.Relu, scale=-1.0)
-        nc.scalar.activation(qp[:].rearrange("p (c i j) -> p c j i", i=4, j=PACK), h_walk, ACT.Relu)
-        nc.scalar.activation(neg_qp[:], qp[:], ACT.Copy, scale=-1.0)
+        nc.scalar.activation(hb[:].rearrange("p (c i j) -> p c j i", i=4, j=PACK), h_walk, ACT.Copy)
+        nc.scalar.activation(qm[:], hb[:], ACT.Relu, scale=-1.0)
         qm_codes = keep.tile([P, V], U32, name="qm_codes", align_bytes=64)
         qp_codes = keep.tile([P, V], U32, name="qp_codes", align_bytes=64)
         qm_scales = keep.tile([P, V], U8, name="qm_scales", align_bytes=64)
@@ -65,19 +64,35 @@ def tile_picked_yquest_gate_p_kernel(tc, x_words, x_scales, e_words, e_scales, h
 
         xs = keep.tile([P, S], U8, name="xs", align_bytes=64)
         es = keep.tile([P, S], U8, name="es", align_bytes=64)
-        ew = keep.tile([P, S], U32, name="ew", align_bytes=64)
-        xw = keep.tile([P, S], U32, name="xw", align_bytes=64)
 
-        nc.vector.tensor_copy(es[:], es_win[:].indirect(offsets[:]))
-        tau_sb = keep.tile([P, 2, 1], F32, name="tau_sb", tag="es_win", align_bytes=64)
+        def half_list(h):
+            return offsets[:, h * HALF // 16 : (h + 1) * HALF // 16]
+
+        def pick_scales(name, window, plane):
+            picked = keep.tile([P, S], U8, name=name, tag=name, align_bytes=64)
+            nc.vector.tensor_copy(picked[:], window[:].indirect(offsets[:]))
+            nc.vector.memset(plane[:].bitcast(I32), 0)
+            for i in range(4):
+                nc.sync.dma_start(plane[i:P:32, :].bitcast(I32), picked[P - 16 + i : P : 4, :].bitcast(I32))
+
+        pick_scales("xs_picked", xs_win, xs)
+        pick_scales("es_picked", es_win, es)
+        tau_sb = keep.tile([P, 2, 1], F32, name="tau_sb", tag="xs_picked", align_bytes=64)
         with nc.allow_non_contiguous_dma(reason="one threshold a partition"):
             nc.sync.dma_start(tau_sb[:], tau.rearrange("(r p) o -> p r o", p=P))
-        nc.vector.tensor_copy(ew[:], ew_win[:].bitcast(U32).indirect(offsets[:]))
-        nc.vector.quantize_mx(out=qm_codes[:].bitcast(FP8X4), scales=qm_scales[:], in_=qm[:])
-        nc.vector.tensor_copy(xw[:], xw_win[:].bitcast(U32).indirect(offsets[:]))
+        tau_shift = keep.tile([P, 2, 1], F32, name="tau_shift")
+        nc.scalar.activation(tau_shift[:], tau_sb[:], ACT.Copy, bias=-LN2)
+        nc.vector.tensor_scalar(neg_qp[:], hb[:], -1.0, 0.0, ALU.mult, ALU.min)
+        xw = [keep.tile([P, HALF], U32, name="xw0", tag="h_raw", align_bytes=64),
+              share.tile([P, HALF], U32, name="xw1", align_bytes=64, offset=0)]
+        ew_all = share.tile([P, S], U32, name="ew_all", align_bytes=64, offset=4 * HALF)
+        ew = [ew_all[:, :HALF], ew_all[:, HALF:]]
+        nc.vector.tensor_copy(xw[0][:], xw_win[:].bitcast(U32).indirect(half_list(0)))
         nc.vector.quantize_mx(out=qp_codes[:].bitcast(FP8X4), scales=qp_scales[:], in_=neg_qp[:])
+        nc.vector.tensor_copy(xw[1][:], xw_win[:].bitcast(U32).indirect(half_list(1)))
+        nc.vector.quantize_mx(out=qm_codes[:].bitcast(FP8X4), scales=qm_scales[:], in_=qm[:])
         for h in range(2):
-            nc.vector.tensor_copy(xs[:, h * HALF : (h + 1) * HALF], xs_win[:].indirect(offsets[:, h * HALF // 16 : (h + 1) * HALF // 16]))
+            nc.vector.tensor_copy(ew[h], ew_win[:].bitcast(U32).indirect(half_list(h)))
 
         banks = {}
         for h in range(2):
@@ -85,74 +100,44 @@ def tile_picked_yquest_gate_p_kernel(tc, x_words, x_scales, e_words, e_scales, h
             for r in range(2):
                 rows = slice(r * P, (r + 1) * P)
                 banks[r, h] = psum.tile([P, HALF], F32, name=f"bank{r}{h}")
-                nc.tensor.matmul_mx(out=banks[r, h][:], lhsT=qm_codes[:, rows].bitcast(FP8X4), lhsT_scale=qm_scales[:, rows],
-                                    rhs=ew[:, cols].bitcast(FP8X4), rhs_scale=es[:, cols], start=True, stop=False)
+                nc.tensor.matmul_mx(out=banks[r, h][:], lhsT=qp_codes[:, rows].bitcast(FP8X4), lhsT_scale=qp_scales[:, rows],
+                                    rhs=xw[h][:].bitcast(FP8X4), rhs_scale=xs[:, cols], start=True, stop=False)
         for h in range(2):
             cols = slice(h * HALF, (h + 1) * HALF)
             for r in range(2):
                 rows = slice(r * P, (r + 1) * P)
-                nc.tensor.matmul_mx(out=banks[r, h][:], lhsT=qp_codes[:, rows].bitcast(FP8X4), lhsT_scale=qp_scales[:, rows],
-                                    rhs=xw[:, cols].bitcast(FP8X4), rhs_scale=xs[:, cols], start=False, stop=True)
+                nc.tensor.matmul_mx(out=banks[r, h][:], lhsT=qm_codes[:, rows].bitcast(FP8X4), lhsT_scale=qm_scales[:, rows],
+                                    rhs=ew[h].bitcast(FP8X4), rhs_scale=es[:, cols], start=False, stop=True)
 
-        low = {}
+        low = [keep.tile([P, 2 * PAIRS], F32, name=f"low{r}") for r in range(2)]
+        lowest = [keep.tile([P, 1], F32, name=f"lowest{r}") for r in range(2)]
         gate = {}
-        weight = {}
-        for r in range(2):
-            low[r, 0] = keep.tile([P, PAIRS], F32, name=f"low{r}0")
-            low[r, 1] = keep.tile([P, PAIRS + 1], F32, name=f"low{r}1")
-        lowest = {}
 
         def pair_min(r, h):
             bank = banks[r, h]
             odd = keep.tile([P, PAIRS], F32, name=f"odd{r}{h}")
-            nc.scalar.copy(odd[:], bank[:, 1::2])
-            nc.vector.tensor_tensor(low[r, h][:, :PAIRS], bank[:, 0::2], odd[:], ALU.min)
-
-        def row_min(r, h):
-            if h == 0:
-                lowest[r, h] = low[r, 1][:, PAIRS:]
-                nc.vector.tensor_reduce(lowest[r, h], low[r, h][:], mybir.AxisListType.X, ALU.min)
-            else:
-                whole = keep.tile([P, 1], F32, name=f"lowest{r}")
-                shifted = keep.tile([P, PAIRS + 1], F32, name=f"shifted{r}")
-                lowest[r, h] = whole[:]
-                nc.vector.tensor_scalar(shifted[:], low[r, h][:], -LN2, None, ALU.add, ALU.min, accum_out=lowest[r, h])
+            nc.scalar.activation(odd[:], bank[:, 1::2], ACT.Copy, bias=-LN2)
+            nc.vector.scalar_tensor_tensor(low[r][:, h * PAIRS : (h + 1) * PAIRS], bank[:, 0::2], -LN2, odd[:], ALU.add, ALU.min)
 
         def tanh(r, h):
             gate[r, h] = keep.tile([P, PAIRS], F32, name=f"gate{r}{h}")
-            nc.scalar.activation(gate[r, h][:], low[r, h][:, :PAIRS], ACT.Tanh, bias=tau_sb[:, r, :], scale=-1.0)
+            nc.scalar.activation(gate[r, h][:], low[r][:, h * PAIRS : (h + 1) * PAIRS], ACT.Tanh, bias=tau_shift[:, r, :], scale=-1.0)
 
-        def exp(r, h):
-            weight[r, h] = keep.tile([P, HALF], F32, name=f"weight{r}{h}")
-            nc.scalar.activation(weight[r, h][:], banks[r, h][:], ACT.Exp, bias=lowest[r, h], scale=-1.0)
+        def finish(r, h):
+            weight = keep.tile([P, HALF], F32, name=f"weight{r}{h}")
+            nc.scalar.activation(weight[:], banks[r, h][:], ACT.Exp, bias=lowest[r][:], scale=-1.0)
+            res = keep.tile([P, HALF], F32, name=f"res{r}{h}")
+            nc.vector.scalar_tensor_tensor(res[:].rearrange("p (v d) -> p v d", d=2), gate[r, h][:].unsqueeze(2).to_broadcast([P, PAIRS, 2]), 1.0,
+                                           weight[:].rearrange("p (v d) -> p v d", d=2), ALU.add, ALU.mult)
+            nc.sync.dma_start(out[r * P : (r + 1) * P, h * HALF : (h + 1) * HALF], res[:])
 
         for r in range(2):
             pair_min(r, 0)
         for r in range(2):
-            row_min(r, 0)
-        for r in range(2):
             pair_min(r, 1)
-        first_gate = {}
+            nc.vector.tensor_reduce(lowest[r][:], low[r][:], mybir.AxisListType.X, ALU.min)
         for r in range(2):
-            tanh(r, 0)
-            exp(r, 0)
-            first_gate[r] = keep.tile([P, PAIRS], F32, name=f"first_gate{r}")
-            nc.gpsimd.tensor_scalar(first_gate[r][:], gate[r, 0][:], 1.0, 1.0, ALU.mult, ALU.add)
-        for r in range(2):
-            row_min(r, 1)
-        for r in range(2):
-            tanh(r, 1)
-        store_queues = [nc.sync, nc.sync, nc.sync, nc.sync]
-        for r in range(2):
-            shrink = keep.tile([P, 1], F32, name=f"shrink{r}")
-            nc.scalar.activation(shrink[:], lowest[r, 0], ACT.Exp, bias=lowest[r, 1], scale=-1.0)
-            exp(r, 1)
             for h in range(2):
-                res = keep.tile([P, HALF], F32, name=f"res{r}{h}")
-                res_pairs = res[:].rearrange("p (v d) -> p v d", d=2)
-                weight_pairs = weight[r, h][:].rearrange("p (v d) -> p v d", d=2)
-                if h == 0:
-                    nc.vector.scalar_tensor_tensor(res_pairs, weight_pairs, shrink[:], first_gate[r][:].unsqueeze(2).to_broadcast([P, PAIRS, 2]), ALU.mult, ALU.mult)
-                else:
-                    nc.vector.scalar_tensor_tensor(res_pairs, gate[r, h][:].unsqueeze(2).to_broadcast([P, PAIRS, 2]), 1.0, weight_pairs, ALU.add, ALU.mult)
-                store_queues[2 * r + h].dma_start(out[r * P : (r + 1) * P, h * HALF : (h + 1) * HALF], res[:])
+                tanh(r, h)
+            for h in range(2):
+                finish(r, h)

@@ -82,14 +82,14 @@ def tile_picked_yquest_gate_p_kernel(tc, x_words, x_scales, e_words, e_scales, h
             nc.sync.dma_start(tau_sb[:], tau.rearrange("(r p) o -> p r o", p=P))
         tau_shift = keep.tile([P, 2, 1], F32, name="tau_shift")
         nc.scalar.activation(tau_shift[:], tau_sb[:], ACT.Copy, bias=-LN2)
-        nc.vector.tensor_scalar(neg_qp[:], hb[:], -1.0, 0.0, ALU.mult, ALU.min)
-        xw = [keep.tile([P, HALF], U32, name="xw0", tag="h_raw", align_bytes=64),
-              share.tile([P, HALF], U32, name="xw1", align_bytes=64, offset=0)]
+        xw = [keep.tile([P, HALF], U32, name="xw0", align_bytes=64),
+              keep.tile([P, HALF], U32, name="xw1", tag="h_raw", align_bytes=64)]
         ew_all = share.tile([P, S], U32, name="ew_all", align_bytes=64, offset=4 * HALF)
         ew = [ew_all[:, :HALF], ew_all[:, HALF:]]
         nc.vector.tensor_copy(xw[0][:], xw_win[:].bitcast(U32).indirect(half_list(0)))
-        nc.vector.quantize_mx(out=qp_codes[:].bitcast(FP8X4), scales=qp_scales[:], in_=neg_qp[:])
+        nc.vector.tensor_scalar(neg_qp[:], hb[:], -1.0, 0.0, ALU.mult, ALU.min)
         nc.vector.tensor_copy(xw[1][:], xw_win[:].bitcast(U32).indirect(half_list(1)))
+        nc.vector.quantize_mx(out=qp_codes[:].bitcast(FP8X4), scales=qp_scales[:], in_=neg_qp[:])
         nc.vector.quantize_mx(out=qm_codes[:].bitcast(FP8X4), scales=qm_scales[:], in_=qm[:])
         for h in range(2):
             nc.vector.tensor_copy(ew[h], ew_win[:].bitcast(U32).indirect(half_list(h)))

@@ -77,11 +77,11 @@ def tile_picked_yquest_gate_p_kernel(tc, x_words, x_scales, e_words, e_scales, h
 
         pick_scales("xs_picked", xs_win, xs)
         pick_scales("es_picked", es_win, es)
-        tau_sb = keep.tile([P, 2, 1], F32, name="tau_sb", tag="xs_picked", align_bytes=64)
+        tau_sb = keep.tile([P, 2, 1], F32, name="tau_sb")
         with nc.allow_non_contiguous_dma(reason="one threshold a partition"):
-            nc.sync.dma_start(tau_sb[:], tau.rearrange("(r p) o -> p r o", p=P))
+            nc.gpsimd.dma_start(tau_sb[:], tau.rearrange("(r p) o -> p r o", p=P))
         tau_shift = keep.tile([P, 2, 1], F32, name="tau_shift")
-        nc.scalar.activation(tau_shift[:], tau_sb[:], ACT.Copy, bias=-LN2)
+        nc.gpsimd.tensor_scalar(tau_shift[:], tau_sb[:], 1.0, -LN2, ALU.mult, ALU.add)
         xw = [keep.tile([P, HALF], U32, name="xw0", align_bytes=64),
               keep.tile([P, HALF], U32, name="xw1", tag="h_raw", align_bytes=64)]
         ew_all = share.tile([P, S], U32, name="ew_all", align_bytes=64, offset=4 * HALF)

@@ -21,6 +21,7 @@ PACK = 4
 HALF = S // 2
 PAIRS = HALF // 2
 LN2 = math.log(2.0)
+LOWEST_F32 = -3.4028234663852886e38
 
 
 def tile_picked_yquest_gate_p_kernel(tc, x_words, x_scales, e_words, e_scales, hT, tau, offs, out):
@@ -28,6 +29,8 @@ def tile_picked_yquest_gate_p_kernel(tc, x_words, x_scales, e_words, e_scales, h
     with ExitStack() as ctx:
         keep = ctx.enter_context(tc.tile_pool(name="keep", bufs=1))
         psum = ctx.enter_context(tc.psum_pool(name="psum", bufs=1))
+
+        share = ctx.enter_context(tc.tile_pool(name="share", bufs=1))
 
         offsets = keep.tile([P, S // 16], U16, name="offsets")
         nc.sync.dma_start(offsets[:], offs)
@@ -43,71 +46,63 @@ def tile_picked_yquest_gate_p_kernel(tc, x_words, x_scales, e_words, e_scales, h
             nc.sync.dma_start(window[:], src[0].rearrange("p n t -> p (n t)").bitcast(I32))
             return window
 
-        xs_win = load_scales("xs_win", x_scales)
         es_win = load_scales("es_win", e_scales)
-        h_raw = keep.tile([P, PACK, V], F32, name="h_raw", tag="h_raw", align_bytes=64)
+        xs_win = load_scales("xs_win", x_scales)
+        h_raw = share.tile([P, PACK, V], F32, name="h_raw", align_bytes=64, offset=0)
         nc.sync.dma_start(h_raw[:], hT.rearrange("(p j) t -> p j t", j=PACK))
-        xw_win = load_words("xw_win", x_words)
         ew_win = load_words("ew_win", e_words)
+        xw_win = load_words("xw_win", x_words)
 
-        qm = keep.tile([P, V * PACK], BF16, name="qm", tag="qm", align_bytes=64)
-        share = ctx.enter_context(tc.tile_pool(name="share", bufs=1))
-        hb = share.tile([P, V * PACK], BF16, name="hb", align_bytes=64, offset=0)
+        qm = keep.tile([P, V * PACK], BF16, name="qm", align_bytes=64)
+        qp = keep.tile([P, V * PACK], BF16, name="qp", tag="qp", align_bytes=64)
         neg_qp = keep.tile([P, V * PACK], BF16, name="neg_qp", align_bytes=64)
         h_walk = h_raw[:].rearrange("p j (c i) -> p c j i", i=4)
-        nc.scalar.activation(hb[:].rearrange("p (c i j) -> p c j i", i=4, j=PACK), h_walk, ACT.Copy)
-        nc.scalar.activation(qm[:], hb[:], ACT.Relu, scale=-1.0)
+        nc.scalar.activation(qm[:].rearrange("p (c i j) -> p c j i", i=4, j=PACK), h_walk, ACT.Relu, scale=-1.0)
+        nc.scalar.activation(qp[:].rearrange("p (c i j) -> p c j i", i=4, j=PACK), h_walk, ACT.Relu)
         qm_codes = keep.tile([P, V], U32, name="qm_codes", align_bytes=64)
         qp_codes = keep.tile([P, V], U32, name="qp_codes", align_bytes=64)
         qm_scales = keep.tile([P, V], U8, name="qm_scales", align_bytes=64)
         qp_scales = keep.tile([P, V], U8, name="qp_scales", align_bytes=64)
 
-        xs = keep.tile([P, S], U8, name="xs", align_bytes=64)
-        es = keep.tile([P, S], U8, name="es", align_bytes=64)
-
         def half_list(h):
             return offsets[:, h * HALF // 16 : (h + 1) * HALF // 16]
 
-        def pick_scales(name, window, plane):
-            picked = keep.tile([P, S], U8, name=name, tag=name, align_bytes=64)
+        def pick_scales(name, window):
+            picked = keep.tile([P, S], U8, name=name + "_picked", tag=name + "_picked", align_bytes=64)
+            plane = keep.tile([P, S], U8, name=name, align_bytes=64)
             nc.vector.tensor_copy(picked[:], window[:].indirect(offsets[:]))
             nc.vector.memset(plane[:].bitcast(I32), 0)
             for i in range(4):
                 nc.sync.dma_start(plane[i:P:32, :].bitcast(I32), picked[P - 16 + i : P : 4, :].bitcast(I32))
+            return plane
 
-        pick_scales("xs_picked", xs_win, xs)
-        pick_scales("es_picked", es_win, es)
-        tau_sb = keep.tile([P, 2, 1], F32, name="tau_sb")
+        es = pick_scales("es", es_win)
+        xs = pick_scales("xs", xs_win)
+        tau_sb = keep.tile([P, 2, 1], F32, name="tau_sb", tag="es_picked", align_bytes=64)
         with nc.allow_non_contiguous_dma(reason="one threshold a partition"):
-            nc.gpsimd.dma_start(tau_sb[:], tau.rearrange("(r p) o -> p r o", p=P))
+            nc.sync.dma_start(tau_sb[:], tau.rearrange("(r p) o -> p r o", p=P))
         tau_shift = keep.tile([P, 2, 1], F32, name="tau_shift")
-        nc.gpsimd.tensor_scalar(tau_shift[:], tau_sb[:], 1.0, -LN2, ALU.mult, ALU.add)
-        xw = [keep.tile([P, HALF], U32, name="xw0", align_bytes=64),
-              keep.tile([P, HALF], U32, name="xw1", tag="h_raw", align_bytes=64)]
-        ew_all = share.tile([P, S], U32, name="ew_all", align_bytes=64, offset=4 * HALF)
-        ew = [ew_all[:, :HALF], ew_all[:, HALF:]]
-        nc.vector.tensor_copy(xw[0][:], xw_win[:].bitcast(U32).indirect(half_list(0)))
-        nc.vector.tensor_scalar(neg_qp[:], hb[:], -1.0, 0.0, ALU.mult, ALU.min)
-        nc.vector.tensor_copy(xw[1][:], xw_win[:].bitcast(U32).indirect(half_list(1)))
-        nc.vector.quantize_mx(out=qp_codes[:].bitcast(FP8X4), scales=qp_scales[:], in_=neg_qp[:])
-        nc.vector.quantize_mx(out=qm_codes[:].bitcast(FP8X4), scales=qm_scales[:], in_=qm[:])
-        for h in range(2):
-            nc.vector.tensor_copy(ew[h], ew_win[:].bitcast(U32).indirect(half_list(h)))
+        nc.scalar.activation(tau_shift[:], tau_sb[:], ACT.Copy, bias=-LN2)
 
-        banks = {}
-        for h in range(2):
-            cols = slice(h * HALF, (h + 1) * HALF)
-            for r in range(2):
-                rows = slice(r * P, (r + 1) * P)
-                banks[r, h] = psum.tile([P, HALF], F32, name=f"bank{r}{h}")
-                nc.tensor.matmul_mx(out=banks[r, h][:], lhsT=qp_codes[:, rows].bitcast(FP8X4), lhsT_scale=qp_scales[:, rows],
-                                    rhs=xw[h][:].bitcast(FP8X4), rhs_scale=xs[:, cols], start=True, stop=False)
-        for h in range(2):
-            cols = slice(h * HALF, (h + 1) * HALF)
-            for r in range(2):
-                rows = slice(r * P, (r + 1) * P)
-                nc.tensor.matmul_mx(out=banks[r, h][:], lhsT=qm_codes[:, rows].bitcast(FP8X4), lhsT_scale=qm_scales[:, rows],
-                                    rhs=ew[h].bitcast(FP8X4), rhs_scale=es[:, cols], start=False, stop=True)
+        ew = keep.tile([P, S], U32, name="ew", align_bytes=64)
+        xw = [share.tile([P, HALF], U32, name="xw0", align_bytes=64, offset=0),
+              keep.tile([P, HALF], U32, name="xw1", tag="qp", align_bytes=64)]
+        nc.vector.tensor_copy(ew[:], ew_win[:].bitcast(U32).indirect(offsets[:]))
+        nc.vector.quantize_mx(out=qm_codes[:].bitcast(FP8X4), scales=qm_scales[:], in_=qm[:])
+        nc.vector.tensor_scalar(neg_qp[:], qp[:], -1.0, None, ALU.mult)
+        nc.vector.tensor_copy(xw[0][:], xw_win[:].bitcast(U32).indirect(half_list(0)))
+        nc.vector.quantize_mx(out=qp_codes[:].bitcast(FP8X4), scales=qp_scales[:], in_=neg_qp[:])
+        nc.vector.tensor_copy(xw[1][:], xw_win[:].bitcast(U32).indirect(half_list(1)))
+
+        banks = {(r, h): psum.tile([P, HALF], F32, name=f"bank{r}{h}") for h in range(2) for r in range(2)}
+        e_side = (qm_codes, qm_scales, [ew[:, :HALF], ew[:, HALF:]], es)
+        x_side = (qp_codes, qp_scales, [xw[0][:], xw[1][:]], xs)
+        for n, (codes, scales, words, plane) in enumerate([e_side, x_side]):
+            for h in range(2):
+                for r in range(2):
+                    rows = slice(r * P, (r + 1) * P)
+                    nc.tensor.matmul_mx(out=banks[r, h][:], lhsT=codes[:, rows].bitcast(FP8X4), lhsT_scale=scales[:, rows],
+                                        rhs=words[h].bitcast(FP8X4), rhs_scale=plane[:, h * HALF : (h + 1) * HALF], start=n == 0, stop=n == 1)
 
         low = [keep.tile([P, 2 * PAIRS], F32, name=f"low{r}") for r in range(2)]
         lowest = [keep.tile([P, 1], F32, name=f"lowest{r}") for r in range(2)]
@@ -131,13 +126,15 @@ def tile_picked_yquest_gate_p_kernel(tc, x_words, x_scales, e_words, e_scales, h
                                            weight[:].rearrange("p (v d) -> p v d", d=2), ALU.add, ALU.mult)
             nc.sync.dma_start(out[r * P : (r + 1) * P, h * HALF : (h + 1) * HALF], res[:])
 
-        for r in range(2):
-            pair_min(r, 0)
-        for r in range(2):
-            pair_min(r, 1)
-            nc.vector.tensor_reduce(lowest[r][:], low[r][:], mybir.AxisListType.X, ALU.min)
+        shifted = keep.tile([P, S], F32, name="shifted")
+        lowest_first = keep.tile([P, 1], F32, name="lowest_first")
+        nc.vector.tensor_scalar(shifted[:, :HALF], banks[0, 0][:], -LN2, None, ALU.add, ALU.min, accum_out=lowest_first[:])
+        nc.vector.tensor_scalar(shifted[:, HALF:], banks[0, 1][:], -LN2, lowest_first[:], ALU.add, ALU.min, accum_out=lowest[0][:])
+        pair_min(1, 0)
+        pair_min(1, 1)
+        nc.vector.tensor_tensor(low[0][:], shifted[:, 0::2], shifted[:, 1::2], ALU.min)
+        nc.vector.tensor_reduce(lowest[1][:], low[1][:], mybir.AxisListType.X, ALU.min)
         for r in range(2):
             for h in range(2):
                 tanh(r, h)
-            for h in range(2):
                 finish(r, h)

@@ -35,10 +35,10 @@ def tile_picked_yquest_gate_p_kernel(tc, x_words, x_scales, e_words, e_scales, h
         offsets = keep.tile([P, S // 16], U16, name="offsets")
         nc.sync.dma_start(offsets[:], offs)
 
-        def load_scales(name, src):
+        def load_scales(name, src, clearer):
             window = keep.tile([P, T], U8, name=name, align_bytes=64)
-            nc.sync.dma_start(window[P - 16 :, :].bitcast(I32), src[0].bitcast(I32))
-            nc.vector.memset(window[: P - 16, :].bitcast(I32), 0)
+            nc.scalar.dma_start(window[P - 16 :, :].bitcast(I32), src[0].bitcast(I32))
+            clearer.memset(window[: P - 16, :].bitcast(I32), 0)
             return window
 
         def load_words(name, src):
@@ -46,8 +46,8 @@ def tile_picked_yquest_gate_p_kernel(tc, x_words, x_scales, e_words, e_scales, h
             nc.sync.dma_start(window[:], src[0].rearrange("p n t -> p (n t)").bitcast(I32))
             return window
 
-        es_win = load_scales("es_win", e_scales)
-        xs_win = load_scales("xs_win", x_scales)
+        es_win = load_scales("es_win", e_scales, nc.vector)
+        xs_win = load_scales("xs_win", x_scales, nc.gpsimd)
         h_raw = share.tile([P, PACK, V], F32, name="h_raw", align_bytes=64, offset=0)
         nc.sync.dma_start(h_raw[:], hT.rearrange("(p j) t -> p j t", j=PACK))
         ew_win = load_words("ew_win", e_words)
@@ -57,8 +57,9 @@ def tile_picked_yquest_gate_p_kernel(tc, x_words, x_scales, e_words, e_scales, h
         qp = keep.tile([P, V * PACK], BF16, name="qp", tag="qp", align_bytes=64)
         neg_qp = keep.tile([P, V * PACK], BF16, name="neg_qp", align_bytes=64)
         h_walk = h_raw[:].rearrange("p j (c i) -> p c j i", i=4)
-        nc.scalar.activation(qm[:].rearrange("p (c i j) -> p c j i", i=4, j=PACK), h_walk, ACT.Relu, scale=-1.0)
         nc.scalar.activation(qp[:].rearrange("p (c i j) -> p c j i", i=4, j=PACK), h_walk, ACT.Relu)
+        nc.gpsimd.tensor_scalar(neg_qp[:], qp[:], -1.0, 0.0, ALU.mult, ALU.add)
+        nc.scalar.activation(qm[:].rearrange("p (c i j) -> p c j i", i=4, j=PACK), h_walk, ACT.Relu, scale=-1.0)
         qm_codes = keep.tile([P, V], U32, name="qm_codes", align_bytes=64)
         qp_codes = keep.tile([P, V], U32, name="qp_codes", align_bytes=64)
         qm_scales = keep.tile([P, V], U8, name="qm_scales", align_bytes=64)
@@ -89,7 +90,6 @@ def tile_picked_yquest_gate_p_kernel(tc, x_words, x_scales, e_words, e_scales, h
               keep.tile([P, HALF], U32, name="xw1", tag="qp", align_bytes=64)]
         nc.vector.tensor_copy(ew[:], ew_win[:].bitcast(U32).indirect(offsets[:]))
         nc.vector.quantize_mx(out=qm_codes[:].bitcast(FP8X4), scales=qm_scales[:], in_=qm[:])
-        nc.vector.tensor_scalar(neg_qp[:], qp[:], -1.0, None, ALU.mult)
         nc.vector.tensor_copy(xw[0][:], xw_win[:].bitcast(U32).indirect(half_list(0)))
         nc.vector.quantize_mx(out=qp_codes[:].bitcast(FP8X4), scales=qp_scales[:], in_=neg_qp[:])
         nc.vector.tensor_copy(xw[1][:], xw_win[:].bitcast(U32).indirect(half_list(1)))
@@ -121,10 +121,14 @@ def tile_picked_yquest_gate_p_kernel(tc, x_words, x_scales, e_words, e_scales, h
         def finish(r, h):
             weight = keep.tile([P, HALF], F32, name=f"weight{r}{h}")
             nc.scalar.activation(weight[:], banks[r, h][:], ACT.Exp, bias=lowest[r][:], scale=-1.0)
-            res = keep.tile([P, HALF], F32, name=f"res{r}{h}")
-            nc.vector.scalar_tensor_tensor(res[:].rearrange("p (v d) -> p v d", d=2), gate[r, h][:].unsqueeze(2).to_broadcast([P, PAIRS, 2]), 1.0,
-                                           weight[:].rearrange("p (v d) -> p v d", d=2), ALU.add, ALU.mult)
-            nc.sync.dma_start(out[r * P : (r + 1) * P, h * HALF : (h + 1) * HALF], res[:])
+            pieces = 2 if (r, h) == (1, 1) else 1
+            width = HALF // pieces
+            for n in range(pieces):
+                res = keep.tile([P, width], F32, name=f"res{r}{h}{n}")
+                nc.vector.scalar_tensor_tensor(res[:].rearrange("p (v d) -> p v d", d=2),
+                                               gate[r, h][:, n * width // 2 : (n + 1) * width // 2].unsqueeze(2).to_broadcast([P, width // 2, 2]), 1.0,
+                                               weight[:, n * width : (n + 1) * width].rearrange("p (v d) -> p v d", d=2), ALU.add, ALU.mult)
+                nc.sync.dma_start(out[r * P : (r + 1) * P, h * HALF + n * width : h * HALF + (n + 1) * width], res[:])
 
         shifted = keep.tile([P, S], F32, name="shifted")
         lowest_first = keep.tile([P, 1], F32, name="lowest_first")

@@ -97,12 +97,11 @@ def tile_picked_yquest_gate_p_kernel(tc, x_words, x_scales, e_words, e_scales, h
         banks = {(r, h): psum.tile([P, HALF], F32, name=f"bank{r}{h}") for h in range(2) for r in range(2)}
         e_side = (qm_codes, qm_scales, [ew[:, :HALF], ew[:, HALF:]], es)
         x_side = (qp_codes, qp_scales, [xw[0][:], xw[1][:]], xs)
-        for n, (codes, scales, words, plane) in enumerate([e_side, x_side]):
-            for h in range(2):
-                for r in range(2):
-                    rows = slice(r * P, (r + 1) * P)
-                    nc.tensor.matmul_mx(out=banks[r, h][:], lhsT=codes[:, rows].bitcast(FP8X4), lhsT_scale=scales[:, rows],
-                                        rhs=words[h].bitcast(FP8X4), rhs_scale=plane[:, h * HALF : (h + 1) * HALF], start=n == 0, stop=n == 1)
+        for n, r, h in [(0, 0, 0), (0, 1, 0), (0, 0, 1), (1, 0, 0), (0, 1, 1), (1, 1, 0), (1, 0, 1), (1, 1, 1)]:
+            codes, scales, words, plane = (e_side, x_side)[n]
+            rows = slice(r * P, (r + 1) * P)
+            nc.tensor.matmul_mx(out=banks[r, h][:], lhsT=codes[:, rows].bitcast(FP8X4), lhsT_scale=scales[:, rows],
+                                rhs=words[h].bitcast(FP8X4), rhs_scale=plane[:, h * HALF : (h + 1) * HALF], start=n == 0, stop=n == 1)
 
         low = [keep.tile([P, 2 * PAIRS], F32, name=f"low{r}") for r in range(2)]
         lowest = [keep.tile([P, 1], F32, name=f"lowest{r}") for r in range(2)]
@@ -132,11 +131,17 @@ def tile_picked_yquest_gate_p_kernel(tc, x_words, x_scales, e_words, e_scales, h
 
         shifted = keep.tile([P, S], F32, name="shifted")
         lowest_first = keep.tile([P, 1], F32, name="lowest_first")
+
+        def pair_min_from_copy(h):
+            cols = shifted[:, h * HALF : (h + 1) * HALF]
+            nc.vector.tensor_tensor(low[0][:, h * PAIRS : (h + 1) * PAIRS], cols[:, 0::2], cols[:, 1::2], ALU.min)
+
         nc.vector.tensor_scalar(shifted[:, :HALF], banks[0, 0][:], -LN2, None, ALU.add, ALU.min, accum_out=lowest_first[:])
+        pair_min_from_copy(0)
         nc.vector.tensor_scalar(shifted[:, HALF:], banks[0, 1][:], -LN2, lowest_first[:], ALU.add, ALU.min, accum_out=lowest[0][:])
         pair_min(1, 0)
         pair_min(1, 1)
-        nc.vector.tensor_tensor(low[0][:], shifted[:, 0::2], shifted[:, 1::2], ALU.min)
+        pair_min_from_copy(1)
         nc.vector.tensor_reduce(lowest[1][:], low[1][:], mybir.AxisListType.X, ALU.min)
         for r in range(2):
             for h in range(2):

@@ -18,10 +18,13 @@ ACT = mybir.ActivationFunctionType
 
 P = 128
 PACK = 4
+QUADRANT = 32
+BLOCKS = K // 32
+GROUP = 16
+LINE = 4
 HALF = S // 2
 PAIRS = HALF // 2
 LN2 = math.log(2.0)
-LOWEST_F32 = -3.4028234663852886e38
 
 
 def tile_picked_yquest_gate_p_kernel(tc, x_words, x_scales, e_words, e_scales, hT, tau, offs, out):
@@ -29,16 +32,15 @@ def tile_picked_yquest_gate_p_kernel(tc, x_words, x_scales, e_words, e_scales, h
     with ExitStack() as ctx:
         keep = ctx.enter_context(tc.tile_pool(name="keep", bufs=1))
         psum = ctx.enter_context(tc.psum_pool(name="psum", bufs=1))
-
         share = ctx.enter_context(tc.tile_pool(name="share", bufs=1))
 
-        offsets = keep.tile([P, S // 16], U16, name="offsets")
+        offsets = keep.tile([P, S // GROUP], U16, name="offsets")
         nc.sync.dma_start(offsets[:], offs)
 
         def load_scales(name, src, clearer):
             window = keep.tile([P, T], U8, name=name, align_bytes=64)
-            nc.scalar.dma_start(window[P - 16 :, :].bitcast(I32), src[0].bitcast(I32))
-            clearer.memset(window[: P - 16, :].bitcast(I32), 0)
+            nc.scalar.dma_start(window[P - BLOCKS :, :].bitcast(I32), src[0].bitcast(I32))
+            clearer.memset(window[: P - BLOCKS, :].bitcast(I32), 0)
             return window
 
         def load_words(name, src):
@@ -56,29 +58,30 @@ def tile_picked_yquest_gate_p_kernel(tc, x_words, x_scales, e_words, e_scales, h
         qm = keep.tile([P, V * PACK], BF16, name="qm", align_bytes=64)
         qp = keep.tile([P, V * PACK], BF16, name="qp", tag="qp", align_bytes=64)
         neg_qp = keep.tile([P, V * PACK], BF16, name="neg_qp", align_bytes=64)
-        h_walk = h_raw[:].rearrange("p j (c i) -> p c j i", i=4)
-        nc.scalar.activation(qp[:].rearrange("p (c i j) -> p c j i", i=4, j=PACK), h_walk, ACT.Relu)
+        h_walk = h_raw[:].rearrange("p j (c i) -> p c j i", i=LINE)
+        nc.scalar.activation(qp[:].rearrange("p (c i j) -> p c j i", i=LINE, j=PACK), h_walk, ACT.Relu)
         nc.gpsimd.tensor_scalar(neg_qp[:], qp[:], -1.0, 0.0, ALU.mult, ALU.add)
-        nc.scalar.activation(qm[:].rearrange("p (c i j) -> p c j i", i=4, j=PACK), h_walk, ACT.Relu, scale=-1.0)
+        nc.scalar.activation(qm[:].rearrange("p (c i j) -> p c j i", i=LINE, j=PACK), h_walk, ACT.Relu, scale=-1.0)
         qm_codes = keep.tile([P, V], U32, name="qm_codes", align_bytes=64)
-        qp_codes = keep.tile([P, V], U32, name="qp_codes", align_bytes=64)
+        neg_qp_codes = keep.tile([P, V], U32, name="neg_qp_codes", align_bytes=64)
         qm_scales = keep.tile([P, V], U8, name="qm_scales", align_bytes=64)
-        qp_scales = keep.tile([P, V], U8, name="qp_scales", align_bytes=64)
+        neg_qp_scales = keep.tile([P, V], U8, name="neg_qp_scales", align_bytes=64)
 
         def half_list(h):
-            return offsets[:, h * HALF // 16 : (h + 1) * HALF // 16]
+            return offsets[:, h * HALF // GROUP : (h + 1) * HALF // GROUP]
 
         def pick_scales(name, window):
             picked = keep.tile([P, S], U8, name=name + "_picked", tag=name + "_picked", align_bytes=64)
             plane = keep.tile([P, S], U8, name=name, align_bytes=64)
             nc.vector.tensor_copy(picked[:], window[:].indirect(offsets[:]))
             nc.vector.memset(plane[:].bitcast(I32), 0)
-            for i in range(4):
-                nc.sync.dma_start(plane[i:P:32, :].bitcast(I32), picked[P - 16 + i : P : 4, :].bitcast(I32))
+            for i in range(PACK):
+                nc.sync.dma_start(plane[i:P:QUADRANT, :].bitcast(I32), picked[P - BLOCKS + i : P : PACK, :].bitcast(I32))
             return plane
 
         es = pick_scales("es", es_win)
         xs = pick_scales("xs", xs_win)
+
         tau_sb = keep.tile([P, 2, 1], F32, name="tau_sb", tag="es_picked", align_bytes=64)
         with nc.allow_non_contiguous_dma(reason="one threshold a partition"):
             nc.sync.dma_start(tau_sb[:], tau.rearrange("(r p) o -> p r o", p=P))
@@ -91,31 +94,33 @@ def tile_picked_yquest_gate_p_kernel(tc, x_words, x_scales, e_words, e_scales, h
         nc.vector.tensor_copy(ew[:], ew_win[:].bitcast(U32).indirect(offsets[:]))
         nc.vector.quantize_mx(out=qm_codes[:].bitcast(FP8X4), scales=qm_scales[:], in_=qm[:])
         nc.vector.tensor_copy(xw[0][:], xw_win[:].bitcast(U32).indirect(half_list(0)))
-        nc.vector.quantize_mx(out=qp_codes[:].bitcast(FP8X4), scales=qp_scales[:], in_=neg_qp[:])
+        nc.vector.quantize_mx(out=neg_qp_codes[:].bitcast(FP8X4), scales=neg_qp_scales[:], in_=neg_qp[:])
         nc.vector.tensor_copy(xw[1][:], xw_win[:].bitcast(U32).indirect(half_list(1)))
 
         banks = {(r, h): psum.tile([P, HALF], F32, name=f"bank{r}{h}") for h in range(2) for r in range(2)}
         e_side = (qm_codes, qm_scales, [ew[:, :HALF], ew[:, HALF:]], es)
-        x_side = (qp_codes, qp_scales, [xw[0][:], xw[1][:]], xs)
-        for n, r, h in [(0, 0, 0), (0, 1, 0), (0, 0, 1), (1, 0, 0), (0, 1, 1), (1, 1, 0), (1, 0, 1), (1, 1, 1)]:
-            codes, scales, words, plane = (e_side, x_side)[n]
-            rows = slice(r * P, (r + 1) * P)
-            nc.tensor.matmul_mx(out=banks[r, h][:], lhsT=codes[:, rows].bitcast(FP8X4), lhsT_scale=scales[:, rows],
-                                rhs=words[h].bitcast(FP8X4), rhs_scale=plane[:, h * HALF : (h + 1) * HALF], start=n == 0, stop=n == 1)
+        x_side = (neg_qp_codes, neg_qp_scales, [xw[0][:], xw[1][:]], xs)
+        for side, (codes, scales, words, plane) in enumerate((e_side, x_side)):
+            for h in range(2):
+                for r in range(2):
+                    rows = slice(r * P, (r + 1) * P)
+                    nc.tensor.matmul_mx(out=banks[r, h][:], lhsT=codes[:, rows].bitcast(FP8X4), lhsT_scale=scales[:, rows],
+                                        rhs=words[h].bitcast(FP8X4), rhs_scale=plane[:, h * HALF : (h + 1) * HALF],
+                                        start=side == 0, stop=side == 1)
 
         low = [keep.tile([P, 2 * PAIRS], F32, name=f"low{r}") for r in range(2)]
         lowest = [keep.tile([P, 1], F32, name=f"lowest{r}") for r in range(2)]
-        gate = {}
+        tanhs = {}
 
-        def pair_min(r, h):
+        def pair_min_from_bank(r, h):
             bank = banks[r, h]
             odd = keep.tile([P, PAIRS], F32, name=f"odd{r}{h}")
             nc.scalar.activation(odd[:], bank[:, 1::2], ACT.Copy, bias=-LN2)
             nc.vector.scalar_tensor_tensor(low[r][:, h * PAIRS : (h + 1) * PAIRS], bank[:, 0::2], -LN2, odd[:], ALU.add, ALU.min)
 
-        def tanh(r, h):
-            gate[r, h] = keep.tile([P, PAIRS], F32, name=f"gate{r}{h}")
-            nc.scalar.activation(gate[r, h][:], low[r][:, h * PAIRS : (h + 1) * PAIRS], ACT.Tanh, bias=tau_shift[:, r, :], scale=-1.0)
+        def gate(r, h):
+            tanhs[r, h] = keep.tile([P, PAIRS], F32, name=f"tanh{r}{h}")
+            nc.scalar.activation(tanhs[r, h][:], low[r][:, h * PAIRS : (h + 1) * PAIRS], ACT.Tanh, bias=tau_shift[:, r, :], scale=-1.0)
 
         def finish(r, h):
             weight = keep.tile([P, HALF], F32, name=f"weight{r}{h}")
@@ -124,8 +129,9 @@ def tile_picked_yquest_gate_p_kernel(tc, x_words, x_scales, e_words, e_scales, h
             width = HALF // pieces
             for n in range(pieces):
                 res = keep.tile([P, width], F32, name=f"res{r}{h}{n}")
+                pair_tanh = tanhs[r, h][:, n * width // 2 : (n + 1) * width // 2]
                 nc.vector.scalar_tensor_tensor(res[:].rearrange("p (v d) -> p v d", d=2),
-                                               gate[r, h][:, n * width // 2 : (n + 1) * width // 2].unsqueeze(2).to_broadcast([P, width // 2, 2]), 1.0,
+                                               pair_tanh.unsqueeze(2).to_broadcast([P, width // 2, 2]), 1.0,
                                                weight[:, n * width : (n + 1) * width].rearrange("p (v d) -> p v d", d=2), ALU.add, ALU.mult)
                 nc.sync.dma_start(out[r * P : (r + 1) * P, h * HALF + n * width : h * HALF + (n + 1) * width], res[:])
 
@@ -139,11 +145,11 @@ def tile_picked_yquest_gate_p_kernel(tc, x_words, x_scales, e_words, e_scales, h
         nc.vector.tensor_scalar(shifted[:, :HALF], banks[0, 0][:], -LN2, None, ALU.add, ALU.min, accum_out=lowest_first[:])
         pair_min_from_copy(0)
         nc.vector.tensor_scalar(shifted[:, HALF:], banks[0, 1][:], -LN2, lowest_first[:], ALU.add, ALU.min, accum_out=lowest[0][:])
-        pair_min(1, 0)
-        pair_min(1, 1)
+        pair_min_from_bank(1, 0)
+        pair_min_from_bank(1, 1)
         pair_min_from_copy(1)
         nc.vector.tensor_reduce(lowest[1][:], low[1][:], mybir.AxisListType.X, ALU.min)
         for r in range(2):
             for h in range(2):
-                tanh(r, h)
+                gate(r, h)
                 finish(r, h)

@@ -23,6 +23,7 @@ BLOCKS = K // 32
 GROUP = 16
 LINE = 4
 HALF = S // 2
+QUARTER = S // 4
 PAIRS = HALF // 2
 LN2 = math.log(2.0)
 
@@ -95,18 +96,26 @@ def tile_picked_yquest_gate_p_kernel(tc, x_words, x_scales, e_words, e_scales, h
         nc.vector.quantize_mx(out=qm_codes[:].bitcast(FP8X4), scales=qm_scales[:], in_=qm[:])
         nc.vector.tensor_copy(xw[0][:], xw_win[:].bitcast(U32).indirect(half_list(0)))
         nc.vector.quantize_mx(out=neg_qp_codes[:].bitcast(FP8X4), scales=neg_qp_scales[:], in_=neg_qp[:])
-        nc.vector.tensor_copy(xw[1][:], xw_win[:].bitcast(U32).indirect(half_list(1)))
+        for n in range(2):
+            first = (HALF + n * QUARTER) // GROUP
+            nc.vector.tensor_copy(xw[1][:, n * QUARTER : (n + 1) * QUARTER], xw_win[:].bitcast(U32).indirect(offsets[:, first : first + QUARTER // GROUP]))
 
         banks = {(r, h): psum.tile([P, HALF], F32, name=f"bank{r}{h}") for h in range(2) for r in range(2)}
-        e_side = (qm_codes, qm_scales, [ew[:, :HALF], ew[:, HALF:]], es)
-        x_side = (neg_qp_codes, neg_qp_scales, [xw[0][:], xw[1][:]], xs)
-        for side, (codes, scales, words, plane) in enumerate((e_side, x_side)):
-            for h in range(2):
-                for r in range(2):
-                    rows = slice(r * P, (r + 1) * P)
-                    nc.tensor.matmul_mx(out=banks[r, h][:], lhsT=codes[:, rows].bitcast(FP8X4), lhsT_scale=scales[:, rows],
-                                        rhs=words[h].bitcast(FP8X4), rhs_scale=plane[:, h * HALF : (h + 1) * HALF],
-                                        start=side == 0, stop=side == 1)
+
+        def multiply(r, codes, scales, words, plane, first, width, start, stop):
+            rows = slice(r * P, (r + 1) * P)
+            h, col = divmod(first, HALF)
+            nc.tensor.matmul_mx(out=banks[r, h][:, col : col + width], lhsT=codes[:, rows].bitcast(FP8X4), lhsT_scale=scales[:, rows],
+                                rhs=words.bitcast(FP8X4), rhs_scale=plane[:, first : first + width], start=start, stop=stop)
+
+        for h in range(2):
+            for r in range(2):
+                multiply(r, qm_codes, qm_scales, ew[:, h * HALF : (h + 1) * HALF], es, h * HALF, HALF, True, False)
+        for r in range(2):
+            multiply(r, neg_qp_codes, neg_qp_scales, xw[0][:], xs, 0, HALF, False, True)
+        for n in range(2):
+            for r in range(2):
+                multiply(r, neg_qp_codes, neg_qp_scales, xw[1][:, n * QUARTER : (n + 1) * QUARTER], xs, HALF + n * QUARTER, QUARTER, False, n == 1)
 
         low = [keep.tile([P, 2 * PAIRS], F32, name=f"low{r}") for r in range(2)]
         lowest = [keep.tile([P, 1], F32, name=f"lowest{r}") for r in range(2)]

@@ -23,7 +23,6 @@ BLOCKS = K // 32
 GROUP = 16
 LINE = 4
 HALF = S // 2
-QUARTER = S // 4
 PAIRS = HALF // 2
 LN2 = math.log(2.0)
 
@@ -56,13 +55,18 @@ def tile_picked_yquest_gate_p_kernel(tc, x_words, x_scales, e_words, e_scales, h
         ew_win = load_words("ew_win", e_words)
         xw_win = load_words("xw_win", x_words)
 
-        qm = keep.tile([P, V * PACK], BF16, name="qm", align_bytes=64)
+        qm = [keep.tile([P, P * PACK], BF16, name=f"qm{r}", tag=f"qm{r}", align_bytes=64) for r in range(2)]
         qp = keep.tile([P, V * PACK], BF16, name="qp", tag="qp", align_bytes=64)
         neg_qp = keep.tile([P, V * PACK], BF16, name="neg_qp", align_bytes=64)
         h_walk = h_raw[:].rearrange("p j (c i) -> p c j i", i=LINE)
-        nc.scalar.activation(qp[:].rearrange("p (c i j) -> p c j i", i=LINE, j=PACK), h_walk, ACT.Relu)
-        nc.gpsimd.tensor_scalar(neg_qp[:], qp[:], -1.0, 0.0, ALU.mult, ALU.add)
-        nc.scalar.activation(qm[:].rearrange("p (c i j) -> p c j i", i=LINE, j=PACK), h_walk, ACT.Relu, scale=-1.0)
+        for r in range(2):
+            nc.scalar.activation(qm[r][:].rearrange("p (c i j) -> p c j i", i=LINE, j=PACK), h_walk[:, r * P // LINE : (r + 1) * P // LINE], ACT.Relu, scale=-1.0)
+        qp_walk = qp[:].rearrange("p (c i j) -> p c j i", i=LINE, j=PACK)
+        for r in range(2):
+            lines = slice(r * P // LINE, (r + 1) * P // LINE)
+            cols = slice(r * P * PACK, (r + 1) * P * PACK)
+            nc.scalar.activation(qp_walk[:, lines], h_walk[:, lines], ACT.Relu)
+            nc.gpsimd.tensor_scalar(neg_qp[:, cols], qp[:, cols], -1.0, 0.0, ALU.mult, ALU.add)
         qm_codes = keep.tile([P, V], U32, name="qm_codes", align_bytes=64)
         neg_qp_codes = keep.tile([P, V], U32, name="neg_qp_codes", align_bytes=64)
         qm_scales = keep.tile([P, V], U8, name="qm_scales", align_bytes=64)
@@ -89,33 +93,27 @@ def tile_picked_yquest_gate_p_kernel(tc, x_words, x_scales, e_words, e_scales, h
         tau_shift = keep.tile([P, 2, 1], F32, name="tau_shift")
         nc.scalar.activation(tau_shift[:], tau_sb[:], ACT.Copy, bias=-LN2)
 
-        ew = keep.tile([P, S], U32, name="ew", align_bytes=64)
+        ew = keep.tile([P, S], U32, name="ew", tag="qm0", align_bytes=64)
         xw = [share.tile([P, HALF], U32, name="xw0", align_bytes=64, offset=0),
               keep.tile([P, HALF], U32, name="xw1", tag="qp", align_bytes=64)]
-        nc.vector.tensor_copy(ew[:], ew_win[:].bitcast(U32).indirect(offsets[:]))
-        nc.vector.quantize_mx(out=qm_codes[:].bitcast(FP8X4), scales=qm_scales[:], in_=qm[:])
+        for r in range(2):
+            nc.vector.quantize_mx(out=qm_codes[:, r * P : (r + 1) * P].bitcast(FP8X4), scales=qm_scales[:, r * P : (r + 1) * P], in_=qm[r][:])
+        for h in range(2):
+            nc.vector.tensor_copy(ew[:, h * HALF : (h + 1) * HALF], ew_win[:].bitcast(U32).indirect(half_list(h)))
         nc.vector.tensor_copy(xw[0][:], xw_win[:].bitcast(U32).indirect(half_list(0)))
         nc.vector.quantize_mx(out=neg_qp_codes[:].bitcast(FP8X4), scales=neg_qp_scales[:], in_=neg_qp[:])
-        for n in range(2):
-            first = (HALF + n * QUARTER) // GROUP
-            nc.vector.tensor_copy(xw[1][:, n * QUARTER : (n + 1) * QUARTER], xw_win[:].bitcast(U32).indirect(offsets[:, first : first + QUARTER // GROUP]))
+        nc.vector.tensor_copy(xw[1][:], xw_win[:].bitcast(U32).indirect(half_list(1)))
 
         banks = {(r, h): psum.tile([P, HALF], F32, name=f"bank{r}{h}") for h in range(2) for r in range(2)}
-
-        def multiply(r, codes, scales, words, plane, first, width, start, stop):
-            rows = slice(r * P, (r + 1) * P)
-            h, col = divmod(first, HALF)
-            nc.tensor.matmul_mx(out=banks[r, h][:, col : col + width], lhsT=codes[:, rows].bitcast(FP8X4), lhsT_scale=scales[:, rows],
-                                rhs=words.bitcast(FP8X4), rhs_scale=plane[:, first : first + width], start=start, stop=stop)
-
-        for h in range(2):
-            for r in range(2):
-                multiply(r, qm_codes, qm_scales, ew[:, h * HALF : (h + 1) * HALF], es, h * HALF, HALF, True, False)
-        for r in range(2):
-            multiply(r, neg_qp_codes, neg_qp_scales, xw[0][:], xs, 0, HALF, False, True)
-        for n in range(2):
-            for r in range(2):
-                multiply(r, neg_qp_codes, neg_qp_scales, xw[1][:, n * QUARTER : (n + 1) * QUARTER], xs, HALF + n * QUARTER, QUARTER, False, n == 1)
+        e_side = (qm_codes, qm_scales, [ew[:, :HALF], ew[:, HALF:]], es)
+        x_side = (neg_qp_codes, neg_qp_scales, [xw[0][:], xw[1][:]], xs)
+        for side, (codes, scales, words, plane) in enumerate((e_side, x_side)):
+            for h in range(2):
+                for r in range(2):
+                    rows = slice(r * P, (r + 1) * P)
+                    nc.tensor.matmul_mx(out=banks[r, h][:], lhsT=codes[:, rows].bitcast(FP8X4), lhsT_scale=scales[:, rows],
+                                        rhs=words[h].bitcast(FP8X4), rhs_scale=plane[:, h * HALF : (h + 1) * HALF],
+                                        start=side == 0, stop=side == 1)
 
         low = [keep.tile([P, 2 * PAIRS], F32, name=f"low{r}") for r in range(2)]
         lowest = [keep.tile([P, 1], F32, name=f"lowest{r}") for r in range(2)]

@@ -61,12 +61,7 @@ def tile_picked_yquest_gate_p_kernel(tc, x_words, x_scales, e_words, e_scales, h
         h_walk = h_raw[:].rearrange("p j (c i) -> p c j i", i=LINE)
         for r in range(2):
             nc.scalar.activation(qm[r][:].rearrange("p (c i j) -> p c j i", i=LINE, j=PACK), h_walk[:, r * P // LINE : (r + 1) * P // LINE], ACT.Relu, scale=-1.0)
-        qp_walk = qp[:].rearrange("p (c i j) -> p c j i", i=LINE, j=PACK)
-        for r in range(2):
-            lines = slice(r * P // LINE, (r + 1) * P // LINE)
-            cols = slice(r * P * PACK, (r + 1) * P * PACK)
-            nc.scalar.activation(qp_walk[:, lines], h_walk[:, lines], ACT.Relu)
-            nc.gpsimd.tensor_scalar(neg_qp[:, cols], qp[:, cols], -1.0, 0.0, ALU.mult, ALU.add)
+        nc.scalar.activation(qp[:].rearrange("p (c i j) -> p c j i", i=LINE, j=PACK), h_walk, ACT.Relu)
         qm_codes = keep.tile([P, V], U32, name="qm_codes", align_bytes=64)
         neg_qp_codes = keep.tile([P, V], U32, name="neg_qp_codes", align_bytes=64)
         qm_scales = keep.tile([P, V], U8, name="qm_scales", align_bytes=64)
@@ -100,6 +95,7 @@ def tile_picked_yquest_gate_p_kernel(tc, x_words, x_scales, e_words, e_scales, h
             nc.vector.quantize_mx(out=qm_codes[:, r * P : (r + 1) * P].bitcast(FP8X4), scales=qm_scales[:, r * P : (r + 1) * P], in_=qm[r][:])
         for h in range(2):
             nc.vector.tensor_copy(ew[:, h * HALF : (h + 1) * HALF], ew_win[:].bitcast(U32).indirect(half_list(h)))
+        nc.vector.tensor_scalar(neg_qp[:], qp[:], -1.0, None, ALU.mult)
         nc.vector.tensor_copy(xw[0][:], xw_win[:].bitcast(U32).indirect(half_list(0)))
         nc.vector.quantize_mx(out=neg_qp_codes[:].bitcast(FP8X4), scales=neg_qp_scales[:], in_=neg_qp[:])
         nc.vector.tensor_copy(xw[1][:], xw_win[:].bitcast(U32).indirect(half_list(1)))

@@ -25,6 +25,7 @@ LINE = 4
 HALF = S // 2
 PAIRS = HALF // 2
 LN2 = math.log(2.0)
+LARGEST = 3.4028234663852886e38
 
 
 def tile_picked_yquest_gate_p_kernel(tc, x_words, x_scales, e_words, e_scales, hT, tau, offs, out):
@@ -61,7 +62,8 @@ def tile_picked_yquest_gate_p_kernel(tc, x_words, x_scales, e_words, e_scales, h
         h_walk = h_raw[:].rearrange("p j (c i) -> p c j i", i=LINE)
         for r in range(2):
             nc.scalar.activation(qm[r][:].rearrange("p (c i j) -> p c j i", i=LINE, j=PACK), h_walk[:, r * P // LINE : (r + 1) * P // LINE], ACT.Relu, scale=-1.0)
-        nc.scalar.activation(qp[:].rearrange("p (c i j) -> p c j i", i=LINE, j=PACK), h_walk, ACT.Relu)
+        nc.gpsimd.tensor_scalar(qp[:].rearrange("p (t j) -> p t j", j=PACK), h_raw[:].rearrange("p j t -> p t j"), LARGEST, 0.0, ALU.min, ALU.max)
+        nc.scalar.activation(neg_qp[:], qp[:], ACT.Copy, scale=-1.0)
         qm_codes = keep.tile([P, V], U32, name="qm_codes", align_bytes=64)
         neg_qp_codes = keep.tile([P, V], U32, name="neg_qp_codes", align_bytes=64)
         qm_scales = keep.tile([P, V], U8, name="qm_scales", align_bytes=64)
@@ -88,20 +90,19 @@ def tile_picked_yquest_gate_p_kernel(tc, x_words, x_scales, e_words, e_scales, h
         tau_shift = keep.tile([P, 2, 1], F32, name="tau_shift")
         nc.scalar.activation(tau_shift[:], tau_sb[:], ACT.Copy, bias=-LN2)
 
-        ew = keep.tile([P, S], U32, name="ew", tag="qm0", align_bytes=64)
+        ew = [keep.tile([P, HALF], U32, name="ew0", align_bytes=64), keep.tile([P, HALF], U32, name="ew1", tag="qm0", align_bytes=64)]
         xw = [share.tile([P, HALF], U32, name="xw0", align_bytes=64, offset=0),
               keep.tile([P, HALF], U32, name="xw1", tag="qp", align_bytes=64)]
+        nc.vector.tensor_copy(ew[0][:], ew_win[:].bitcast(U32).indirect(half_list(0)))
         for r in range(2):
             nc.vector.quantize_mx(out=qm_codes[:, r * P : (r + 1) * P].bitcast(FP8X4), scales=qm_scales[:, r * P : (r + 1) * P], in_=qm[r][:])
-        for h in range(2):
-            nc.vector.tensor_copy(ew[:, h * HALF : (h + 1) * HALF], ew_win[:].bitcast(U32).indirect(half_list(h)))
-        nc.vector.tensor_scalar(neg_qp[:], qp[:], -1.0, None, ALU.mult)
+        nc.vector.tensor_copy(ew[1][:], ew_win[:].bitcast(U32).indirect(half_list(1)))
         nc.vector.tensor_copy(xw[0][:], xw_win[:].bitcast(U32).indirect(half_list(0)))
         nc.vector.quantize_mx(out=neg_qp_codes[:].bitcast(FP8X4), scales=neg_qp_scales[:], in_=neg_qp[:])
         nc.vector.tensor_copy(xw[1][:], xw_win[:].bitcast(U32).indirect(half_list(1)))
 
         banks = {(r, h): psum.tile([P, HALF], F32, name=f"bank{r}{h}") for h in range(2) for r in range(2)}
-        e_side = (qm_codes, qm_scales, [ew[:, :HALF], ew[:, HALF:]], es)
+        e_side = (qm_codes, qm_scales, [ew[0][:], ew[1][:]], es)
         x_side = (neg_qp_codes, neg_qp_scales, [xw[0][:], xw[1][:]], xs)
         for side, (codes, scales, words, plane) in enumerate((e_side, x_side)):
             for h in range(2):

@@ -72,19 +72,25 @@ def tile_picked_yquest_gate_p_kernel(tc, x_words, x_scales, e_words, e_scales, h
         def half_list(h):
             return offsets[:, h * HALF // GROUP : (h + 1) * HALF // GROUP]
 
-        def pick_scales(name, window):
-            picked = keep.tile([P, S], U8, name=name + "_picked", tag=name + "_picked", align_bytes=64)
-            plane = keep.tile([P, S], U8, name=name, align_bytes=64)
-            nc.vector.tensor_copy(picked[:], window[:].indirect(offsets[:]))
-            nc.vector.memset(plane[:].bitcast(I32), 0)
-            for i in range(PACK):
-                nc.sync.dma_start(plane[i:P:QUADRANT, :].bitcast(I32), picked[P - BLOCKS + i : P : PACK, :].bitcast(I32))
-            return plane
+        picked = keep.tile([P, 2 * S], U8, name="picked", align_bytes=64)
+        plane = keep.tile([P, 2 * S], U8, name="plane", align_bytes=64)
+        nc.vector.memset(plane[:].bitcast(I32), 0)
 
-        es = pick_scales("es", es_win)
-        xs = pick_scales("xs", xs_win)
+        def move(i, first, end):
+            nc.sync.dma_start(plane[i:P:QUADRANT, first:end].bitcast(I32), picked[P - BLOCKS + i : P : PACK, first:end].bitcast(I32))
 
-        tau_sb = keep.tile([P, 2, 1], F32, name="tau_sb", tag="es_picked", align_bytes=64)
+        nc.vector.tensor_copy(picked[:, :S], es_win[:].indirect(offsets[:]))
+        for i in range(PACK - 1):
+            move(i, 0, S)
+        nc.vector.tensor_copy(picked[:, S : S + HALF], xs_win[:].indirect(half_list(0)))
+        move(PACK - 1, 0, S + HALF)
+        nc.vector.tensor_copy(picked[:, S + HALF :], xs_win[:].indirect(half_list(1)))
+        for i in range(PACK - 1):
+            move(i, S, 2 * S)
+        move(PACK - 1, S + HALF, 2 * S)
+        es, xs = plane[:, :S], plane[:, S:]
+
+        tau_sb = keep.tile([P, 2, 1], F32, name="tau_sb", tag="xs_win", align_bytes=64)
         with nc.allow_non_contiguous_dma(reason="one threshold a partition"):
             nc.sync.dma_start(tau_sb[:], tau.rearrange("(r p) o -> p r o", p=P))
         tau_shift = keep.tile([P, 2, 1], F32, name="tau_shift")
@@ -104,12 +110,12 @@ def tile_picked_yquest_gate_p_kernel(tc, x_words, x_scales, e_words, e_scales, h
         banks = {(r, h): psum.tile([P, HALF], F32, name=f"bank{r}{h}") for h in range(2) for r in range(2)}
         e_side = (qm_codes, qm_scales, [ew[0][:], ew[1][:]], es)
         x_side = (neg_qp_codes, neg_qp_scales, [xw[0][:], xw[1][:]], xs)
-        for side, (codes, scales, words, plane) in enumerate((e_side, x_side)):
+        for side, (codes, scales, words, page_scales) in enumerate((e_side, x_side)):
             for h in range(2):
                 for r in range(2):
                     rows = slice(r * P, (r + 1) * P)
                     nc.tensor.matmul_mx(out=banks[r, h][:], lhsT=codes[:, rows].bitcast(FP8X4), lhsT_scale=scales[:, rows],
-                                        rhs=words[h].bitcast(FP8X4), rhs_scale=plane[:, h * HALF : (h + 1) * HALF],
+                                        rhs=words[h].bitcast(FP8X4), rhs_scale=page_scales[:, h * HALF : (h + 1) * HALF],
                                         start=side == 0, stop=side == 1)
 
         low = [keep.tile([P, 2 * PAIRS], F32, name=f"low{r}") for r in range(2)]

@@ -23,6 +23,7 @@ BLOCKS = K // 32
 GROUP = 16
 LINE = 4
 HALF = S // 2
+QUARTER = S // 4
 PAIRS = HALF // 2
 LN2 = math.log(2.0)
 LARGEST = 3.4028234663852886e38
@@ -105,18 +106,26 @@ def tile_picked_yquest_gate_p_kernel(tc, x_words, x_scales, e_words, e_scales, h
         nc.vector.tensor_copy(ew[1][:], ew_win[:].bitcast(U32).indirect(half_list(1)))
         nc.vector.tensor_copy(xw[0][:], xw_win[:].bitcast(U32).indirect(half_list(0)))
         nc.vector.quantize_mx(out=neg_qp_codes[:].bitcast(FP8X4), scales=neg_qp_scales[:], in_=neg_qp[:])
-        nc.vector.tensor_copy(xw[1][:], xw_win[:].bitcast(U32).indirect(half_list(1)))
+        for n in range(2):
+            first = (HALF + n * QUARTER) // GROUP
+            nc.vector.tensor_copy(xw[1][:, n * QUARTER : (n + 1) * QUARTER], xw_win[:].bitcast(U32).indirect(offsets[:, first : first + QUARTER // GROUP]))
 
         banks = {(r, h): psum.tile([P, HALF], F32, name=f"bank{r}{h}") for h in range(2) for r in range(2)}
-        e_side = (qm_codes, qm_scales, [ew[0][:], ew[1][:]], es)
-        x_side = (neg_qp_codes, neg_qp_scales, [xw[0][:], xw[1][:]], xs)
-        for side, (codes, scales, words, page_scales) in enumerate((e_side, x_side)):
-            for h in range(2):
-                for r in range(2):
-                    rows = slice(r * P, (r + 1) * P)
-                    nc.tensor.matmul_mx(out=banks[r, h][:], lhsT=codes[:, rows].bitcast(FP8X4), lhsT_scale=scales[:, rows],
-                                        rhs=words[h].bitcast(FP8X4), rhs_scale=page_scales[:, h * HALF : (h + 1) * HALF],
-                                        start=side == 0, stop=side == 1)
+
+        def multiply(r, codes, scales, words, page_scales, first, width, start, stop):
+            rows = slice(r * P, (r + 1) * P)
+            h, col = divmod(first, HALF)
+            nc.tensor.matmul_mx(out=banks[r, h][:, col : col + width], lhsT=codes[:, rows].bitcast(FP8X4), lhsT_scale=scales[:, rows],
+                                rhs=words.bitcast(FP8X4), rhs_scale=page_scales[:, first : first + width], start=start, stop=stop)
+
+        for h in range(2):
+            for r in range(2):
+                multiply(r, qm_codes, qm_scales, ew[h][:], es, h * HALF, HALF, True, False)
+        for r in range(2):
+            multiply(r, neg_qp_codes, neg_qp_scales, xw[0][:], xs, 0, HALF, False, True)
+        for n in range(2):
+            for r in range(2):
+                multiply(r, neg_qp_codes, neg_qp_scales, xw[1][:, n * QUARTER : (n + 1) * QUARTER], xs, HALF + n * QUARTER, QUARTER, False, n == 1)
 
         low = [keep.tile([P, 2 * PAIRS], F32, name=f"low{r}") for r in range(2)]
         lowest = [keep.tile([P, 1], F32, name=f"lowest{r}") for r in range(2)]

@@ -142,16 +142,16 @@ def tile_picked_yquest_gate_p_kernel(tc, x_words, x_scales, e_words, e_scales, h
             nc.scalar.activation(tanhs[r, h][:], low[r][:, h * PAIRS : (h + 1) * PAIRS], ACT.Tanh, bias=tau_shift[:, r, :], scale=-1.0)
 
         def finish(r, h):
-            weight = keep.tile([P, HALF], F32, name=f"weight{r}{h}")
-            nc.scalar.activation(weight[:], banks[r, h][:], ACT.Exp, bias=lowest[r][:], scale=-1.0)
             pieces = 2 if (r, h) == (1, 1) else 1
             width = HALF // pieces
             for n in range(pieces):
+                weight = keep.tile([P, width], F32, name=f"weight{r}{h}{n}")
+                nc.scalar.activation(weight[:], banks[r, h][:, n * width : (n + 1) * width], ACT.Exp, bias=lowest[r][:], scale=-1.0)
                 res = keep.tile([P, width], F32, name=f"res{r}{h}{n}")
                 pair_tanh = tanhs[r, h][:, n * width // 2 : (n + 1) * width // 2]
                 nc.vector.scalar_tensor_tensor(res[:].rearrange("p (v d) -> p v d", d=2),
                                                pair_tanh.unsqueeze(2).to_broadcast([P, width // 2, 2]), 1.0,
-                                               weight[:, n * width : (n + 1) * width].rearrange("p (v d) -> p v d", d=2), ALU.add, ALU.mult)
+                                               weight[:].rearrange("p (v d) -> p v d", d=2), ALU.add, ALU.mult)
                 nc.sync.dma_start(out[r * P : (r + 1) * P, h * HALF + n * width : h * HALF + (n + 1) * width], res[:])
 
         shifted = keep.tile([P, S], F32, name="shifted")

@@ -57,12 +57,11 @@ def tile_picked_yquest_gate_p_kernel(tc, x_words, x_scales, e_words, e_scales, h
         ew_win = load_words("ew_win", e_words)
         xw_win = load_words("xw_win", x_words)
 
-        qm = [keep.tile([P, P * PACK], BF16, name=f"qm{r}", tag=f"qm{r}", align_bytes=64) for r in range(2)]
+        qm = keep.tile([P, V * PACK], BF16, name="qm", align_bytes=64)
         qp = keep.tile([P, V * PACK], BF16, name="qp", tag="qp", align_bytes=64)
         neg_qp = keep.tile([P, V * PACK], BF16, name="neg_qp", align_bytes=64)
         h_walk = h_raw[:].rearrange("p j (c i) -> p c j i", i=LINE)
-        for r in range(2):
-            nc.scalar.activation(qm[r][:].rearrange("p (c i j) -> p c j i", i=LINE, j=PACK), h_walk[:, r * P // LINE : (r + 1) * P // LINE], ACT.Relu, scale=-1.0)
+        nc.scalar.activation(qm[:].rearrange("p (c i j) -> p c j i", i=LINE, j=PACK), h_walk, ACT.Relu, scale=-1.0)
         nc.gpsimd.tensor_scalar(qp[:].rearrange("p (t j) -> p t j", j=PACK), h_raw[:].rearrange("p j t -> p t j"), LARGEST, 0.0, ALU.min, ALU.max)
         nc.scalar.activation(neg_qp[:], qp[:], ACT.Copy, scale=-1.0)
         qm_codes = keep.tile([P, V], U32, name="qm_codes", align_bytes=64)
@@ -97,12 +96,11 @@ def tile_picked_yquest_gate_p_kernel(tc, x_words, x_scales, e_words, e_scales, h
         tau_shift = keep.tile([P, 2, 1], F32, name="tau_shift")
         nc.scalar.activation(tau_shift[:], tau_sb[:], ACT.Copy, bias=-LN2)
 
-        ew = [keep.tile([P, HALF], U32, name="ew0", align_bytes=64), keep.tile([P, HALF], U32, name="ew1", tag="qm0", align_bytes=64)]
+        ew = [keep.tile([P, HALF], U32, name="ew0", align_bytes=64), share.tile([P, HALF], U32, name="ew1", align_bytes=64, offset=HALF * 4)]
         xw = [share.tile([P, HALF], U32, name="xw0", align_bytes=64, offset=0),
               keep.tile([P, HALF], U32, name="xw1", tag="qp", align_bytes=64)]
         nc.vector.tensor_copy(ew[0][:], ew_win[:].bitcast(U32).indirect(half_list(0)))
-        for r in range(2):
-            nc.vector.quantize_mx(out=qm_codes[:, r * P : (r + 1) * P].bitcast(FP8X4), scales=qm_scales[:, r * P : (r + 1) * P], in_=qm[r][:])
+        nc.vector.quantize_mx(out=qm_codes[:].bitcast(FP8X4), scales=qm_scales[:], in_=qm[:])
         nc.vector.tensor_copy(ew[1][:], ew_win[:].bitcast(U32).indirect(half_list(1)))
         nc.vector.tensor_copy(xw[0][:], xw_win[:].bitcast(U32).indirect(half_list(0)))
         nc.vector.quantize_mx(out=neg_qp_codes[:].bitcast(FP8X4), scales=neg_qp_scales[:], in_=neg_qp[:])
@@ -142,7 +140,7 @@ def tile_picked_yquest_gate_p_kernel(tc, x_words, x_scales, e_words, e_scales, h
             nc.scalar.activation(tanhs[r, h][:], low[r][:, h * PAIRS : (h + 1) * PAIRS], ACT.Tanh, bias=tau_shift[:, r, :], scale=-1.0)
 
         def finish(r, h):
-            pieces = 2 if (r, h) == (1, 1) else 1
+            pieces = 1 + r
             width = HALF // pieces
             for n in range(pieces):
                 weight = keep.tile([P, width], F32, name=f"weight{r}{h}{n}")

@@ -21,6 +21,7 @@ PACK = 4
 QUADRANT = 32
 BLOCKS = K // 32
 GROUP = 16
+WORD_BYTES = 4
 LINE = 4
 HALF = S // 2
 QUARTER = S // 4
@@ -62,7 +63,8 @@ def tile_picked_yquest_gate_p_kernel(tc, x_words, x_scales, e_words, e_scales, h
         neg_qp = keep.tile([P, V * PACK], BF16, name="neg_qp", align_bytes=64)
         h_walk = h_raw[:].rearrange("p j (c i) -> p c j i", i=LINE)
         nc.scalar.activation(qm[:].rearrange("p (c i j) -> p c j i", i=LINE, j=PACK), h_walk, ACT.Relu, scale=-1.0)
-        nc.gpsimd.tensor_scalar(qp[:].rearrange("p (t j) -> p t j", j=PACK), h_raw[:].rearrange("p j t -> p t j"), LARGEST, 0.0, ALU.min, ALU.max)
+        nc.gpsimd.tensor_scalar(qp[:].rearrange("p (t j) -> p t j", j=PACK), h_raw[:].rearrange("p j t -> p t j"),
+                                LARGEST, 0.0, ALU.min, ALU.max)
         nc.scalar.activation(neg_qp[:], qp[:], ACT.Copy, scale=-1.0)
         qm_codes = keep.tile([P, V], U32, name="qm_codes", align_bytes=64)
         neg_qp_codes = keep.tile([P, V], U32, name="neg_qp_codes", align_bytes=64)
@@ -77,7 +79,8 @@ def tile_picked_yquest_gate_p_kernel(tc, x_words, x_scales, e_words, e_scales, h
         nc.vector.memset(plane[:].bitcast(I32), 0)
 
         def move(i, first, end):
-            nc.sync.dma_start(plane[i:P:QUADRANT, first:end].bitcast(I32), picked[P - BLOCKS + i : P : PACK, first:end].bitcast(I32))
+            nc.sync.dma_start(plane[i:P:QUADRANT, first:end].bitcast(I32),
+                              picked[P - BLOCKS + i : P : PACK, first:end].bitcast(I32))
 
         nc.vector.tensor_copy(picked[:, :S], es_win[:].indirect(offsets[:]))
         for i in range(PACK - 1):
@@ -94,9 +97,10 @@ def tile_picked_yquest_gate_p_kernel(tc, x_words, x_scales, e_words, e_scales, h
         with nc.allow_non_contiguous_dma(reason="one threshold a partition"):
             nc.sync.dma_start(tau_sb[:], tau.rearrange("(r p) o -> p r o", p=P))
         tau_shift = keep.tile([P, 2, 1], F32, name="tau_shift")
-        nc.scalar.activation(tau_shift[:], tau_sb[:], ACT.Copy, bias=-LN2)
+        nc.gpsimd.tensor_scalar(tau_shift[:], tau_sb[:], -LN2, 1.0, ALU.add, ALU.mult)
 
-        ew = [keep.tile([P, HALF], U32, name="ew0", align_bytes=64), share.tile([P, HALF], U32, name="ew1", align_bytes=64, offset=HALF * 4)]
+        ew = [keep.tile([P, HALF], U32, name="ew0", align_bytes=64),
+              share.tile([P, HALF], U32, name="ew1", align_bytes=64, offset=HALF * WORD_BYTES)]
         xw = [share.tile([P, HALF], U32, name="xw0", align_bytes=64, offset=0),
               keep.tile([P, HALF], U32, name="xw1", tag="qp", align_bytes=64)]
         nc.vector.tensor_copy(ew[0][:], ew_win[:].bitcast(U32).indirect(half_list(0)))
@@ -105,16 +109,19 @@ def tile_picked_yquest_gate_p_kernel(tc, x_words, x_scales, e_words, e_scales, h
         nc.vector.tensor_copy(xw[0][:], xw_win[:].bitcast(U32).indirect(half_list(0)))
         nc.vector.quantize_mx(out=neg_qp_codes[:].bitcast(FP8X4), scales=neg_qp_scales[:], in_=neg_qp[:])
         for n in range(2):
-            first = (HALF + n * QUARTER) // GROUP
-            nc.vector.tensor_copy(xw[1][:, n * QUARTER : (n + 1) * QUARTER], xw_win[:].bitcast(U32).indirect(offsets[:, first : first + QUARTER // GROUP]))
+            column = (HALF + n * QUARTER) // GROUP
+            nc.vector.tensor_copy(xw[1][:, n * QUARTER : (n + 1) * QUARTER],
+                                  xw_win[:].bitcast(U32).indirect(offsets[:, column : column + QUARTER // GROUP]))
 
         banks = {(r, h): psum.tile([P, HALF], F32, name=f"bank{r}{h}") for h in range(2) for r in range(2)}
 
         def multiply(r, codes, scales, words, page_scales, first, width, start, stop):
             rows = slice(r * P, (r + 1) * P)
             h, col = divmod(first, HALF)
-            nc.tensor.matmul_mx(out=banks[r, h][:, col : col + width], lhsT=codes[:, rows].bitcast(FP8X4), lhsT_scale=scales[:, rows],
-                                rhs=words.bitcast(FP8X4), rhs_scale=page_scales[:, first : first + width], start=start, stop=stop)
+            nc.tensor.matmul_mx(out=banks[r, h][:, col : col + width],
+                                lhsT=codes[:, rows].bitcast(FP8X4), lhsT_scale=scales[:, rows],
+                                rhs=words.bitcast(FP8X4), rhs_scale=page_scales[:, first : first + width],
+                                start=start, stop=stop)
 
         for h in range(2):
             for r in range(2):
@@ -123,7 +130,8 @@ def tile_picked_yquest_gate_p_kernel(tc, x_words, x_scales, e_words, e_scales, h
             multiply(r, neg_qp_codes, neg_qp_scales, xw[0][:], xs, 0, HALF, False, True)
         for n in range(2):
             for r in range(2):
-                multiply(r, neg_qp_codes, neg_qp_scales, xw[1][:, n * QUARTER : (n + 1) * QUARTER], xs, HALF + n * QUARTER, QUARTER, False, n == 1)
+                multiply(r, neg_qp_codes, neg_qp_scales, xw[1][:, n * QUARTER : (n + 1) * QUARTER], xs,
+                         HALF + n * QUARTER, QUARTER, False, n == 1)
 
         low = [keep.tile([P, 2 * PAIRS], F32, name=f"low{r}") for r in range(2)]
         lowest = [keep.tile([P, 1], F32, name=f"lowest{r}") for r in range(2)]
@@ -140,7 +148,7 @@ def tile_picked_yquest_gate_p_kernel(tc, x_words, x_scales, e_words, e_scales, h
             nc.scalar.activation(tanhs[r, h][:], low[r][:, h * PAIRS : (h + 1) * PAIRS], ACT.Tanh, bias=tau_shift[:, r, :], scale=-1.0)
 
         def finish(r, h):
-            pieces = 1 + r
+            pieces = 2 if r == 1 else 1
             width = HALF // pieces
             for n in range(pieces):
                 weight = keep.tile([P, width], F32, name=f"weight{r}{h}{n}")

@@ -59,13 +59,15 @@ def tile_picked_yquest_gate_p_kernel(tc, x_words, x_scales, e_words, e_scales, h
         xw_win = load_words("xw_win", x_words)
 
         qm = keep.tile([P, V * PACK], BF16, name="qm", align_bytes=64)
-        qp = keep.tile([P, V * PACK], BF16, name="qp", tag="qp", align_bytes=64)
-        neg_qp = keep.tile([P, V * PACK], BF16, name="neg_qp", align_bytes=64)
+        qp = [share.tile([P, P * PACK], BF16, name=f"qp{r}", align_bytes=64, offset=(PACK * V + r * HALF) * WORD_BYTES) for r in range(2)]
+        neg_qp = [keep.tile([P, P * PACK], BF16, name=f"neg_qp{r}", align_bytes=64) for r in range(2)]
         h_walk = h_raw[:].rearrange("p j (c i) -> p c j i", i=LINE)
         nc.scalar.activation(qm[:].rearrange("p (c i j) -> p c j i", i=LINE, j=PACK), h_walk, ACT.Relu, scale=-1.0)
-        nc.gpsimd.tensor_scalar(qp[:].rearrange("p (t j) -> p t j", j=PACK), h_raw[:].rearrange("p j t -> p t j"),
-                                LARGEST, 0.0, ALU.min, ALU.max)
-        nc.scalar.activation(neg_qp[:], qp[:], ACT.Copy, scale=-1.0)
+        for r in range(2):
+            nc.gpsimd.tensor_scalar(qp[r][:].rearrange("p (t j) -> p t j", j=PACK),
+                                    h_raw[:, :, r * P : (r + 1) * P].rearrange("p j t -> p t j"), LARGEST, 0.0, ALU.min, ALU.max)
+        for r in range(2):
+            nc.scalar.activation(neg_qp[r][:], qp[r][:], ACT.Copy, scale=-1.0)
         qm_codes = keep.tile([P, V], U32, name="qm_codes", align_bytes=64)
         neg_qp_codes = keep.tile([P, V], U32, name="neg_qp_codes", align_bytes=64)
         qm_scales = keep.tile([P, V], U8, name="qm_scales", align_bytes=64)
@@ -101,13 +103,18 @@ def tile_picked_yquest_gate_p_kernel(tc, x_words, x_scales, e_words, e_scales, h
 
         ew = [keep.tile([P, HALF], U32, name="ew0", align_bytes=64),
               share.tile([P, HALF], U32, name="ew1", align_bytes=64, offset=HALF * WORD_BYTES)]
-        xw = [share.tile([P, HALF], U32, name="xw0", align_bytes=64, offset=0),
-              keep.tile([P, HALF], U32, name="xw1", tag="qp", align_bytes=64)]
+        xw = [share.tile([P, HALF], U32, name=f"xw{h}", align_bytes=64, offset=(PACK * V + HALF + h * HALF) * WORD_BYTES - 64) for h in range(2)]
+
+        def quantise_neg_qp(r):
+            rows = slice(r * P, (r + 1) * P)
+            nc.vector.quantize_mx(out=neg_qp_codes[:, rows].bitcast(FP8X4), scales=neg_qp_scales[:, rows], in_=neg_qp[r][:])
+
         nc.vector.tensor_copy(ew[0][:], ew_win[:].bitcast(U32).indirect(half_list(0)))
         nc.vector.quantize_mx(out=qm_codes[:].bitcast(FP8X4), scales=qm_scales[:], in_=qm[:])
         nc.vector.tensor_copy(ew[1][:], ew_win[:].bitcast(U32).indirect(half_list(1)))
+        quantise_neg_qp(0)
         nc.vector.tensor_copy(xw[0][:], xw_win[:].bitcast(U32).indirect(half_list(0)))
-        nc.vector.quantize_mx(out=neg_qp_codes[:].bitcast(FP8X4), scales=neg_qp_scales[:], in_=neg_qp[:])
+        quantise_neg_qp(1)
         for n in range(2):
             column = (HALF + n * QUARTER) // GROUP
             nc.vector.tensor_copy(xw[1][:, n * QUARTER : (n + 1) * QUARTER],

from contextlib import ExitStack
import math

import concourse.mybir as mybir

K, T, S, V = 512, 1024, 512, 256
FLOPS = 2 * 2 * K * V * S

F32 = mybir.dt.float32
BF16 = mybir.dt.bfloat16
I32 = mybir.dt.int32
U32 = mybir.dt.uint32
U16 = mybir.dt.uint16
U8 = mybir.dt.uint8
FP8X4 = mybir.dt.float8_e4m3fn_x4
ALU = mybir.AluOpType
ACT = mybir.ActivationFunctionType

P = 128
PACK = 4
QUADRANT = 32
BLOCKS = K // 32
GROUP = 16
WORD_BYTES = 4
LINE = 4
HALF = S // 2
QUARTER = S // 4
PAIRS = HALF // 2
LN2 = math.log(2.0)
LARGEST = 3.4028234663852886e38


def tile_picked_yquest_gate_p_kernel(tc, x_words, x_scales, e_words, e_scales, hT, tau, offs, out):
    nc = tc.nc
    with ExitStack() as ctx:
        keep = ctx.enter_context(tc.tile_pool(name="keep", bufs=1))
        psum = ctx.enter_context(tc.psum_pool(name="psum", bufs=1))
        share = ctx.enter_context(tc.tile_pool(name="share", bufs=1))

        offsets = keep.tile([P, S // GROUP], U16, name="offsets")
        nc.sync.dma_start(offsets[:], offs)

        def load_scales(name, src, clearer):
            window = keep.tile([P, T], U8, name=name, align_bytes=64)
            nc.scalar.dma_start(window[P - BLOCKS :, :].bitcast(I32), src[0].bitcast(I32))
            clearer.memset(window[: P - BLOCKS, :].bitcast(I32), 0)
            return window

        def load_words(name, src):
            window = keep.tile([P, T], I32, name=name, align_bytes=64)
            nc.sync.dma_start(window[:], src[0].rearrange("p n t -> p (n t)").bitcast(I32))
            return window

        es_win = load_scales("es_win", e_scales, nc.vector)
        xs_win = load_scales("xs_win", x_scales, nc.gpsimd)
        h_raw = share.tile([P, PACK, V], F32, name="h_raw", align_bytes=64, offset=0)
        nc.sync.dma_start(h_raw[:], hT.rearrange("(p j) t -> p j t", j=PACK))
        ew_win = load_words("ew_win", e_words)
        xw_win = load_words("xw_win", x_words)

        qm = keep.tile([P, V * PACK], BF16, name="qm", align_bytes=64)
        qp = [share.tile([P, P * PACK], BF16, name=f"qp{r}", align_bytes=64, offset=(PACK * V + r * HALF) * WORD_BYTES) for r in range(2)]
        neg_qp = [keep.tile([P, P * PACK], BF16, name=f"neg_qp{r}", align_bytes=64) for r in range(2)]
        h_walk = h_raw[:].rearrange("p j (c i) -> p c j i", i=LINE)
        nc.scalar.activation(qm[:].rearrange("p (c i j) -> p c j i", i=LINE, j=PACK), h_walk, ACT.Relu, scale=-1.0)
        for r in range(2):
            nc.gpsimd.tensor_scalar(qp[r][:].rearrange("p (t j) -> p t j", j=PACK),
                                    h_raw[:, :, r * P : (r + 1) * P].rearrange("p j t -> p t j"), LARGEST, 0.0, ALU.min, ALU.max)
        for r in range(2):
            nc.scalar.activation(neg_qp[r][:], qp[r][:], ACT.Copy, scale=-1.0)
        qm_codes = keep.tile([P, V], U32, name="qm_codes", align_bytes=64)
        neg_qp_codes = keep.tile([P, V], U32, name="neg_qp_codes", align_bytes=64)
        qm_scales = keep.tile([P, V], U8, name="qm_scales", align_bytes=64)
        neg_qp_scales = keep.tile([P, V], U8, name="neg_qp_scales", align_bytes=64)

        def half_list(h):
            return offsets[:, h * HALF // GROUP : (h + 1) * HALF // GROUP]

        picked = keep.tile([P, 2 * S], U8, name="picked", align_bytes=64)
        plane = keep.tile([P, 2 * S], U8, name="plane", align_bytes=64)
        nc.vector.memset(plane[:].bitcast(I32), 0)

        def move(i, first, end):
            nc.sync.dma_start(plane[i:P:QUADRANT, first:end].bitcast(I32),
                              picked[P - BLOCKS + i : P : PACK, first:end].bitcast(I32))

        nc.vector.tensor_copy(picked[:, :S], es_win[:].indirect(offsets[:]))
        for i in range(PACK - 1):
            move(i, 0, S)
        nc.vector.tensor_copy(picked[:, S : S + HALF], xs_win[:].indirect(half_list(0)))
        move(PACK - 1, 0, S + HALF)
        nc.vector.tensor_copy(picked[:, S + HALF :], xs_win[:].indirect(half_list(1)))
        for i in range(PACK - 1):
            move(i, S, 2 * S)
        move(PACK - 1, S + HALF, 2 * S)
        es, xs = plane[:, :S], plane[:, S:]

        tau_sb = keep.tile([P, 2, 1], F32, name="tau_sb", tag="xs_win", align_bytes=64)
        with nc.allow_non_contiguous_dma(reason="one threshold a partition"):
            nc.sync.dma_start(tau_sb[:], tau.rearrange("(r p) o -> p r o", p=P))
        tau_shift = keep.tile([P, 2, 1], F32, name="tau_shift")
        nc.gpsimd.tensor_scalar(tau_shift[:], tau_sb[:], -LN2, 1.0, ALU.add, ALU.mult)

        ew = [keep.tile([P, HALF], U32, name="ew0", align_bytes=64),
              share.tile([P, HALF], U32, name="ew1", align_bytes=64, offset=HALF * WORD_BYTES)]
        xw = [share.tile([P, HALF], U32, name=f"xw{h}", align_bytes=64, offset=(PACK * V + HALF + h * HALF) * WORD_BYTES - 64) for h in range(2)]

        def quantise_neg_qp(r):
            rows = slice(r * P, (r + 1) * P)
            nc.vector.quantize_mx(out=neg_qp_codes[:, rows].bitcast(FP8X4), scales=neg_qp_scales[:, rows], in_=neg_qp[r][:])

        nc.vector.tensor_copy(ew[0][:], ew_win[:].bitcast(U32).indirect(half_list(0)))
        nc.vector.quantize_mx(out=qm_codes[:].bitcast(FP8X4), scales=qm_scales[:], in_=qm[:])
        nc.vector.tensor_copy(ew[1][:], ew_win[:].bitcast(U32).indirect(half_list(1)))
        quantise_neg_qp(0)
        nc.vector.tensor_copy(xw[0][:], xw_win[:].bitcast(U32).indirect(half_list(0)))
        quantise_neg_qp(1)
        for n in range(2):
            column = (HALF + n * QUARTER) // GROUP
            nc.vector.tensor_copy(xw[1][:, n * QUARTER : (n + 1) * QUARTER],
                                  xw_win[:].bitcast(U32).indirect(offsets[:, column : column + QUARTER // GROUP]))

        banks = {(r, h): psum.tile([P, HALF], F32, name=f"bank{r}{h}") for h in range(2) for r in range(2)}

        def multiply(r, codes, scales, words, page_scales, first, width, start, stop):
            rows = slice(r * P, (r + 1) * P)
            h, col = divmod(first, HALF)
            nc.tensor.matmul_mx(out=banks[r, h][:, col : col + width],
                                lhsT=codes[:, rows].bitcast(FP8X4), lhsT_scale=scales[:, rows],
                                rhs=words.bitcast(FP8X4), rhs_scale=page_scales[:, first : first + width],
                                start=start, stop=stop)

        for h in range(2):
            for r in range(2):
                multiply(r, qm_codes, qm_scales, ew[h][:], es, h * HALF, HALF, True, False)
        for r in range(2):
            multiply(r, neg_qp_codes, neg_qp_scales, xw[0][:], xs, 0, HALF, False, True)
        for n in range(2):
            for r in range(2):
                multiply(r, neg_qp_codes, neg_qp_scales, xw[1][:, n * QUARTER : (n + 1) * QUARTER], xs,
                         HALF + n * QUARTER, QUARTER, False, n == 1)

        low = [keep.tile([P, 2 * PAIRS], F32, name=f"low{r}") for r in range(2)]
        lowest = [keep.tile([P, 1], F32, name=f"lowest{r}") for r in range(2)]
        tanhs = {}

        def pair_min_from_bank(r, h):
            bank = banks[r, h]
            odd = keep.tile([P, PAIRS], F32, name=f"odd{r}{h}")
            nc.scalar.activation(odd[:], bank[:, 1::2], ACT.Copy, bias=-LN2)
            nc.vector.scalar_tensor_tensor(low[r][:, h * PAIRS : (h + 1) * PAIRS], bank[:, 0::2], -LN2, odd[:], ALU.add, ALU.min)

        def gate(r, h):
            tanhs[r, h] = keep.tile([P, PAIRS], F32, name=f"tanh{r}{h}")
            nc.scalar.activation(tanhs[r, h][:], low[r][:, h * PAIRS : (h + 1) * PAIRS], ACT.Tanh, bias=tau_shift[:, r, :], scale=-1.0)

        def finish(r, h):
            pieces = 2 if r == 1 else 1
            width = HALF // pieces
            for n in range(pieces):
                weight = keep.tile([P, width], F32, name=f"weight{r}{h}{n}")
                nc.scalar.activation(weight[:], banks[r, h][:, n * width : (n + 1) * width], ACT.Exp, bias=lowest[r][:], scale=-1.0)
                res = keep.tile([P, width], F32, name=f"res{r}{h}{n}")
                pair_tanh = tanhs[r, h][:, n * width // 2 : (n + 1) * width // 2]
                nc.vector.scalar_tensor_tensor(res[:].rearrange("p (v d) -> p v d", d=2),
                                               pair_tanh.unsqueeze(2).to_broadcast([P, width // 2, 2]), 1.0,
                                               weight[:].rearrange("p (v d) -> p v d", d=2), ALU.add, ALU.mult)
                nc.sync.dma_start(out[r * P : (r + 1) * P, h * HALF + n * width : h * HALF + (n + 1) * width], res[:])

        shifted = keep.tile([P, S], F32, name="shifted")
        lowest_first = keep.tile([P, 1], F32, name="lowest_first")

        def pair_min_from_copy(h):
            cols = shifted[:, h * HALF : (h + 1) * HALF]
            nc.vector.tensor_tensor(low[0][:, h * PAIRS : (h + 1) * PAIRS], cols[:, 0::2], cols[:, 1::2], ALU.min)

        nc.vector.tensor_scalar(shifted[:, :HALF], banks[0, 0][:], -LN2, None, ALU.add, ALU.min, accum_out=lowest_first[:])
        pair_min_from_copy(0)
        nc.vector.tensor_scalar(shifted[:, HALF:], banks[0, 1][:], -LN2, lowest_first[:], ALU.add, ALU.min, accum_out=lowest[0][:])
        pair_min_from_bank(1, 0)
        pair_min_from_bank(1, 1)
        pair_min_from_copy(1)
        nc.vector.tensor_reduce(lowest[1][:], low[1][:], mybir.AxisListType.X, ALU.min)
        for r in range(2):
            for h in range(2):
                gate(r, h)
                finish(r, h)
